import numpy as np
import ml_dtypes


def mxq(x, axis, fmt="e4m3"):
    dtype, down = {"e4m3": (ml_dtypes.float8_e4m3fn, 7), "e5m2": (ml_dtypes.float8_e5m2, 14)}[fmt]
    v = np.moveaxis(np.asarray(x, np.float32).astype(ml_dtypes.bfloat16).astype(np.float64), axis, -1)
    blocks = v.reshape(v.shape[:-1] + (-1, 32))
    amax = np.abs(blocks).max(-1, keepdims=True)
    byte = np.maximum(np.where(amax > 0, np.frexp(amax)[1] - 1 + 127, 0) - down, 1)
    scale = np.exp2(byte - 127.0)
    codes = (blocks / scale).astype(np.float32).astype(dtype).astype(np.float64)
    return np.moveaxis((codes * scale).reshape(v.shape), -1, axis)


WIDE = False


def mx_kscale(k):
    if not WIDE:
        return np.ones(k)
    levels = np.array([10, -10, 5, -5, 0])
    if k % 512:
        return np.exp2(np.random.permutation(np.resize(levels, k // 32))).repeat(32)
    a = np.empty((k // 512, 16))
    for p in range(k // 512):
        a[p, :8] = np.random.permutation(np.resize(levels, 8))
        for g in range(8):
            far = levels[np.abs(levels - a[p, g]) >= 10]
            a[p, g + 8] = far[np.random.randint(len(far))]
    return np.exp2(a.ravel()).repeat(32)


BF16 = ml_dtypes.bfloat16


def bf(x):
    return np.asarray(x, np.float32).astype(BF16)


def f64(x):
    return np.asarray(x).astype(np.float64)

def planes(Y):
    n, m = Y.shape
    b = f64(bf(Y)).reshape(n // 32, 32, m)
    amax = np.abs(b).max(1)
    byte = np.clip(np.where(amax > 0, np.frexp(amax)[1] - 1 + 127 - 7, 1), 1, 254)
    codes = (b * np.exp2(127.0 - byte)[:, None, :]).reshape(n, m).astype(np.float32).astype(ml_dtypes.float8_e4m3fn).view(np.uint8)
    words = codes.reshape(n // 512, 128, 4, m).transpose(0, 1, 3, 2)
    return np.ascontiguousarray(words), np.ascontiguousarray(byte.astype(np.uint8).reshape(n // 512, 16, m))


P, R, M, N = 1024, 1024, 1024, 1024


def setup_inputs():
    s, t = mx_kscale(M), mx_kscale(R)
    return {
        "j": bf(np.random.standard_normal((R, M)) * s[None, :]),
        "red": bf(np.random.standard_normal((N, M)) / np.sqrt(M) / s[None, :]),
        "phi": bf(np.random.uniform(0.5, 1.5, N)),
        "eps": bf(np.random.uniform(0.2, 0.8, R)),
        "b": bf(np.random.standard_normal((R, N))),
        "kappa": bf((1.0 + 0.1 * np.random.standard_normal(R)) * t),
        "lam": bf(np.random.standard_normal((P, R)) / np.sqrt(R) / t[None, :]),
    }


def scattering_integral(j, red):
    return mxq(j, 1, "e4m3") @ mxq(red, 1, "e4m3").T


def line_source(sc, phi, eps, b):
    e = eps[:, None]
    return (1.0 - e) * sc / phi[None, :] + e * b


def core(j, red, phi, eps, b, kappa, lam):
    sc = scattering_integral(f64(j), f64(red))
    s = line_source(sc, f64(phi), f64(eps), f64(b))
    eta = f64(kappa)[:, None] * s
    return mxq(f64(lam), 1, "e4m3") @ mxq(eta, 0, "e4m3")


def reference(j, red, phi, eps, b, kappa, lam):
    R_out = core(j, red, phi, eps, b, kappa, lam)
    words, scales = planes(R_out)
    return R_out, words, scales

@@ -1,0 +1,392 @@
+from contextlib import ExitStack
+
+import concourse.mybir as mybir
+from concourse.masks import make_identity
+
+F32 = mybir.dt.float32
+BF16 = mybir.dt.bfloat16
+U32 = mybir.dt.uint32
+I32 = mybir.dt.int32
+U8 = mybir.dt.uint8
+FP8X4 = mybir.dt.float8_e4m3fn_x4
+ALU = mybir.AluOpType
+ACT = mybir.ActivationFunctionType
+
+P = 128
+D = 1024
+T = 4
+G = 2
+H = 2
+NH = 512
+FLOPS = 2 * 2 * D * D * D
+
+
+def tile_redistributedsourcesharedoperatorstep_kernel(
+    tc, j, red, phi, eps, b, kappa, lam, out_0, out_1, out_2
+):
+    nc = tc.nc
+    with ExitStack() as ctx:
+        keep = ctx.enter_context(tc.tile_pool(name="keep", bufs=1))
+        raw = ctx.enter_context(tc.tile_pool(name="raw", bufs=1))
+        grp = ctx.enter_context(tc.tile_pool(name="grp", bufs=3))
+        mid = ctx.enter_context(tc.tile_pool(name="mid", bufs=2))
+        res = ctx.enter_context(tc.tile_pool(name="res", bufs=2))
+        psum = ctx.enter_context(tc.psum_pool(name="psum", bufs=4))
+        ctx.enter_context(tc.manual_schedule())
+
+        eps_sb = keep.tile([P, G * T], BF16, name="eps_sb")
+        kap_sb = keep.tile([P, G * T], BF16, name="kap_sb")
+        phi_sb = keep.tile([P, 8], BF16, name="phi_sb")
+        nc.scalar.dma_start(out=phi_sb[:], in_=phi.rearrange("(k i) -> k i", i=8))
+        nc.scalar.dma_start(
+            out=eps_sb[:].rearrange("p (g t) -> p g t", g=G),
+            in_=eps.rearrange("(g p t) -> p g t", g=G, t=T),
+        )
+        nc.scalar.dma_start(
+            out=kap_sb[:].rearrange("p (g t) -> p g t", g=G),
+            in_=kappa.rearrange("(g p t) -> p g t", g=G, t=T),
+        )
+
+        red_raw = raw.tile([P, 8, D], BF16, name="red_raw")
+        j_raw = raw.tile([P, G, T, D], BF16, name="j_raw")
+        lam_raw = raw.tile([P, G, T, D], BF16, name="lam_raw")
+        b_raw = raw.tile([P, G, T, D], BF16, name="b_raw")
+
+        def load_red(i):
+            nc.sync.dma_start(out=red_raw[:, i, :], in_=red[P * i : P * (i + 1), :])
+
+        def load4(dst, src, g, t0, t1, c0=0, c1=D):
+            nc.sync.dma_start(
+                out=dst[:, g, t0:t1, c0:c1],
+                in_=src[512 * g : 512 * (g + 1), :].rearrange("(p t) k -> p t k", t=T)[:, t0:t1, c0:c1],
+            )
+
+        for i in range(4):
+            load_red(i)
+        for t in range(T):
+            load4(j_raw, j, 0, t, t + 1)
+        load4(b_raw, b, 0, 0, T, 0, NH)
+        load4(j_raw, j, 1, 0, 2)
+        load4(j_raw, j, 1, 2, 4)
+        load4(b_raw, b, 1, 0, T, 0, NH)
+        for i in range(4, 8):
+            load_red(i)
+        load4(b_raw, b, 0, 0, T, NH, D)
+        load4(b_raw, b, 1, 0, T, NH, D)
+        load4(lam_raw, lam, 0, 0, 2)
+        load4(lam_raw, lam, 0, 2, 4)
+        load4(lam_raw, lam, 1, 0, 2)
+        load4(lam_raw, lam, 1, 2, 4)
+
+        ident = keep.tile([P, P], F32, name="ident")
+        make_identity(nc, ident[:])
+
+        fac_a = keep.tile([P, G * T], F32, name="fac_a")
+        fac_b = keep.tile([P, G * T], F32, name="fac_b")
+        one_m = keep.tile([P, G * T], F32, name="one_m")
+        nc.gpsimd.tensor_scalar(out=one_m[:], in0=eps_sb[:], scalar1=-1.0, scalar2=1.0, op0=ALU.mult, op1=ALU.add)
+        nc.gpsimd.tensor_tensor(out=fac_a[:], in0=kap_sb[:], in1=one_m[:], op=ALU.mult)
+        nc.gpsimd.tensor_tensor(out=fac_b[:], in0=kap_sb[:], in1=eps_sb[:], op=ALU.mult)
+        inv_col = keep.tile([P, 8], F32, name="inv_col")
+        nc.vector.reciprocal(out=inv_col[:], in_=phi_sb[:])
+        inv_phi = keep.tile([P, D], F32, name="inv_phi")
+
+        red_c = [keep.tile([P, G, NH], U32, name=f"red_c{h}", align_bytes=64) for h in range(H)]
+        red_s = [keep.tile([P, G, NH], U8, name=f"red_s{h}", align_bytes=64) for h in range(H)]
+        j_c = [keep.tile([P, T, G, P], U32, name=f"j_c{g}", align_bytes=64) for g in range(G)]
+        j_s = [keep.tile([P, T, G, P], U8, name=f"j_s{g}", align_bytes=64) for g in range(G)]
+        lam_c = [keep.tile([P, T, G, P], U32, name=f"lam_c{g}", align_bytes=64) for g in range(G)]
+        lam_s = [keep.tile([P, T, G, P], U8, name=f"lam_s{g}", align_bytes=64) for g in range(G)]
+        eta_c = [[keep.tile([P, NH], U32, name=f"eta_c{g}{h}", align_bytes=64) for h in range(H)] for g in range(G)]
+        eta_s = [[keep.tile([P, NH], U8, name=f"eta_s{g}{h}", align_bytes=64) for h in range(H)] for g in range(G)]
+        out_c = [[keep.tile([P, NH], U32, name=f"out_c{g}{h}", align_bytes=64) for h in range(H)] for g in range(G)]
+        out_s = [keep.tile([P, G, NH], U8, name=f"out_s{h}", align_bytes=64) for h in range(H)]
+
+        def turn(src, dst, eng="s"):
+            ps = psum.tile([P, G * 2, P], F32, name="turn_ps", tag="tp")
+            words = src.bitcast(F32)
+            for g in range(G):
+                for u in range(2):
+                    nc.tensor.transpose(ps[:, 2 * g + u, :], words[:, 256 * g + u : 256 * (g + 1) : 2], ident[:])
+            src_ps = ps[:].rearrange("p (g u) r -> p g r u", u=2)
+            if eng == "s":
+                nc.scalar.copy(out=dst, in_=src_ps)
+            else:
+                nc.vector.tensor_copy(out=dst, in_=src_ps)
+
+        def word_view(tile4096, g_outer):
+            flat = tile4096[:].bitcast(F32)
+            if g_outer:
+                return flat.rearrange("p (g n u) -> p g n u", g=G, u=2)
+            return flat.rearrange("p (t g n u) -> p t g n u", t=T, g=G, u=2)
+
+
+        def turn_red(tile, i):
+            turn(red_raw[:, i, :], word_view(tile, True)[:, :, P * (i % 4) : P * (i % 4 + 1), :])
+
+        def quant_red(tile, h, pair):
+            src = tile[:].rearrange("p (g w) -> p g w", g=G)
+            for g in range(G):
+                nc.vector.quantize_mx(
+                    out=red_c[h][:, g, 256 * pair : 256 * (pair + 1)].bitcast(FP8X4),
+                    scales=red_s[h][:, g, 256 * pair : 256 * (pair + 1)],
+                    in_=src[:, g, 1024 * pair : 1024 * (pair + 1)],
+                )
+
+        def turn_slot(raw_tile, tile, g, t):
+            turn(raw_tile[:, g, t, :], word_view(tile, False)[:, t, :, :, :])
+
+        def quant_slot(tile, codes, scales, t0, t1):
+            nc.vector.quantize_mx(
+                out=codes[:, t0:t1].rearrange("p t g m -> p (t g m)").bitcast(FP8X4),
+                scales=scales[:, t0:t1].rearrange("p t g m -> p (t g m)"),
+                in_=tile[:, 1024 * t0 : 1024 * t1],
+            )
+
+        def stage1(r, h, t, banks):
+            ps = psum.tile([P, NH], F32, name="mm_ps", tag="mm")
+            for g in range(G):
+                nc.tensor.matmul_mx(
+                    out=ps[:],
+                    lhsT=j_c[r][:, t, g, :].bitcast(FP8X4),
+                    lhsT_scale=j_s[r][:, t, g, :],
+                    rhs=red_c[h][:, g, :].bitcast(FP8X4),
+                    rhs_scale=red_s[h][:, g, :],
+                    start=(g == 0),
+                    stop=(g == G - 1),
+                )
+            banks[t] = ps
+
+        def scale_bank(r, h, t, banks, u):
+            k = T * r + t
+            nc.vector.scalar_tensor_tensor(
+                out=u[:, t, :], in0=banks[t][:], scalar=fac_a[:, k : k + 1],
+                in1=inv_phi[:, NH * h : NH * (h + 1)], op0=ALU.mult, op1=ALU.mult,
+            )
+
+        def new_w(r, h):
+            return mid.tile([P, T, NH], F32, name=f"w{r}{h}", tag="w", bufs=3)
+
+        def thermal(w, r, h, t, eng):
+            k = T * r + t
+            src = b_raw[:, r, t, NH * h : NH * (h + 1)]
+            if eng == "s":
+                nc.scalar.activation(out=w[:, t, :], in_=src, func=ACT.Copy, scale=fac_b[:, k : k + 1])
+            else:
+                nc.vector.tensor_scalar(out=w[:, t, :], in0=src, scalar1=fac_b[:, k : k + 1], scalar2=None, op0=ALU.mult)
+
+        def add_eta(u, w):
+            eta = mid.tile([P, NH * T], BF16, name="eta", tag="eta", align_bytes=64)
+            nc.vector.tensor_tensor(
+                out=eta[:].rearrange("p (c i t) -> p c t i", i=4, t=T),
+                in0=u[:].rearrange("p t (c i) -> p c t i", i=4),
+                in1=w[:].rearrange("p t (c i) -> p c t i", i=4),
+                op=ALU.add,
+            )
+            return eta
+
+        def quant_eta(eta, r, h):
+            nc.vector.quantize_mx(out=eta_c[r][h][:].bitcast(FP8X4), scales=eta_s[r][h][:], in_=eta[:])
+
+        def pass2(ps, q, h, t, r):
+            nc.tensor.matmul_mx(
+                out=ps[:],
+                lhsT=lam_c[q][:, t, r, :].bitcast(FP8X4),
+                lhsT_scale=lam_s[q][:, t, r, :],
+                rhs=eta_c[r][h][:].bitcast(FP8X4),
+                rhs_scale=eta_s[r][h][:],
+                start=(r == 0),
+                stop=(r == G - 1),
+            )
+
+        def empty(o, ps, t, eng):
+            if eng == "s":
+                nc.scalar.copy(out=o[:, t, :], in_=ps[:])
+            else:
+                nc.vector.tensor_copy(out=o[:, t, :], in_=ps[:])
+
+        def store_out(o, q, h, t0, t1):
+            nc.sync.dma_start(
+                out=out_0[512 * q : 512 * (q + 1), :].rearrange("(p t) n -> p t n", t=T)[:, t0:t1, NH * h : NH * (h + 1)],
+                in_=o[:, t0:t1, :],
+            )
+
+        def weave_out(o, eng):
+            oq = res.tile([P, NH * T], BF16, name="oq", tag="oq", align_bytes=64)
+            dst = oq[:].rearrange("p (c i t) -> p c t i", i=4, t=T)
+            src = o[:].rearrange("p t (c i) -> p c t i", i=4)
+            if eng == "s":
+                nc.scalar.copy(out=dst, in_=src)
+            else:
+                nc.vector.tensor_copy(out=dst, in_=src)
+            return oq
+
+        def quant_out(oq, q, h):
+            nc.vector.quantize_mx(out=out_c[q][h][:].bitcast(FP8X4), scales=out_s[h][:, q, :], in_=oq[:])
+
+        def store_codes(q, h):
+            nc.sync.dma_start(
+                out=out_1[q].rearrange("p m t -> p (m t)").bitcast(I32)[:, NH * h : NH * (h + 1)],
+                in_=out_c[q][h][:].bitcast(I32),
+            )
+
+        def store_scales(h):
+            for quad in range(4):
+                nc.sync.dma_start(
+                    out=out_2[:, 4 * quad : 4 * quad + 4, NH * h : NH * (h + 1)].rearrange("g q n -> q g n").bitcast(I32),
+                    in_=out_s[h][32 * quad : 32 * quad + 4, :, :].bitcast(I32),
+                )
+
+        def group_tile(name):
+            return grp.tile([P, T * D], BF16, name=name, tag="grp", align_bytes=64)
+
+        def new_u(r, h):
+            return mid.tile([P, T, NH], F32, name=f"u{r}{h}", tag="u")
+
+        def new_o(q, h):
+            return res.tile([P, T, NH], F32, name=f"o{q}{h}", tag="o", bufs=3)
+
+        def new_bank(tag):
+            return psum.tile([P, NH], F32, name="out_ps", tag=tag)
+
+        def turn4(raw_tile, tile, g):
+            for t in range(T):
+                turn_slot(raw_tile, tile, g, t)
+
+        for half in range(2):
+            ps = psum.tile([P, 4, P], F32, name="phi_ps", tag="mm")
+            for i in range(4):
+                k = 4 * half + i
+                nc.tensor.transpose(ps[:, i, :], inv_col[:, k : k + 1].to_broadcast([P, P]), ident[:])
+            nc.vector.tensor_copy(
+                out=inv_phi[:].rearrange("p (k i) -> p k i", i=8)[:, :, 4 * half : 4 * half + 4],
+                in_=ps[:].rearrange("p i k -> p k i"),
+            )
+        gr0 = group_tile("gr0")
+        turn_red(gr0, 0)
+        turn_red(gr0, 1)
+        quant_red(gr0, 0, 0)
+        turn_red(gr0, 2)
+        turn_red(gr0, 3)
+        quant_red(gr0, 0, 1)
+        gj0 = group_tile("gj0")
+        u00 = new_u(0, 0)
+        w00 = new_w(0, 0)
+        banks = {}
+        for t in range(4):
+            turn_slot(j_raw, gj0, 0, t)
+            quant_slot(gj0, j_c[0], j_s[0], t, t + 1)
+        for t in range(4):
+            stage1(0, 0, t, banks)
+        for t in range(T):
+            thermal(w00, 0, 0, t, "s" if t < 2 else "v")
+            scale_bank(0, 0, t, banks, u00)
+        gj1 = group_tile("gj1")
+        turn4(j_raw, gj1, 1)
+        quant_slot(gj1, j_c[1], j_s[1], 0, 2)
+        eta00 = add_eta(u00, w00)
+        quant_slot(gj1, j_c[1], j_s[1], 2, 4)
+        banks = {}
+        u10 = new_u(1, 0)
+        w10 = new_w(1, 0)
+        for t in range(T):
+            thermal(w10, 1, 0, t, "s")
+        gr1 = group_tile("gr1")
+        for i in range(4):
+            turn_red(gr1, 4 + i)
+        for t in range(T):
+            stage1(1, 0, t, banks)
+        scale_bank(1, 0, 0, banks, u10)
+        scale_bank(1, 0, 1, banks, u10)
+        quant_eta(eta00, 0, 0)
+        scale_bank(1, 0, 2, banks, u10)
+        scale_bank(1, 0, 3, banks, u10)
+        quant_red(gr1, 1, 0)
+        quant_red(gr1, 1, 1)
+        eta10 = add_eta(u10, w10)
+        u01 = new_u(0, 1)
+        w01 = new_w(0, 1)
+        for t in range(T):
+            thermal(w01, 0, 1, t, "s")
+        gl0 = group_tile("gl0")
+        turn4(lam_raw, gl0, 0)
+        banks = {}
+        for t in range(T):
+            stage1(0, 1, t, banks)
+        scale_bank(0, 1, 0, banks, u01)
+        scale_bank(0, 1, 1, banks, u01)
+        quant_eta(eta10, 1, 0)
+        scale_bank(0, 1, 2, banks, u01)
+        scale_bank(0, 1, 3, banks, u01)
+        quant_slot(gl0, lam_c[0], lam_s[0], 0, 2)
+        eta01 = add_eta(u01, w01)
+        quant_slot(gl0, lam_c[0], lam_s[0], 2, 4)
+        banks = {}
+        u11 = new_u(1, 1)
+        w11 = new_w(1, 1)
+        gl1 = group_tile("gl1")
+        turn4(lam_raw, gl1, 1)
+        for t in range(T):
+            stage1(1, 1, t, banks)
+        for t in range(T):
+            thermal(w11, 1, 1, t, "s")
+        scale_bank(1, 1, 0, banks, u11)
+        scale_bank(1, 1, 1, banks, u11)
+        quant_eta(eta01, 0, 1)
+        scale_bank(1, 1, 2, banks, u11)
+        scale_bank(1, 1, 3, banks, u11)
+        quant_slot(gl1, lam_c[1], lam_s[1], 0, 2)
+        quant_slot(gl1, lam_c[1], lam_s[1], 2, 4)
+        eta11 = add_eta(u11, w11)
+
+        o00 = new_o(0, 0)
+        for t in range(T):
+            ps = new_bank("tp")
+            pass2(ps, 0, 0, t, 0)
+            pass2(ps, 0, 0, t, 1)
+            empty(o00, ps, t, "s")
+        store_out(o00, 0, 0, 0, T)
+        o10 = new_o(1, 0)
+        for t in range(T):
+            ps = new_bank("tp")
+            pass2(ps, 1, 0, t, 0)
+            pass2(ps, 1, 0, t, 1)
+            empty(o10, ps, t, "s")
+        store_out(o10, 1, 0, 0, T)
+        oq00 = weave_out(o00, "s")
+        quant_eta(eta11, 1, 1)
+        bank01 = []
+        for t in range(T):
+            ps = new_bank("mm")
+            pass2(ps, 0, 1, t, 0)
+            bank01.append(ps)
+        bank11 = []
+        for t in range(T):
+            ps = new_bank("tp")
+            pass2(ps, 1, 1, t, 0)
+            bank11.append(ps)
+        oq10 = weave_out(o10, "v")
+        quant_out(oq00, 0, 0)
+        store_codes(0, 0)
+        quant_out(oq10, 1, 0)
+        store_codes(1, 0)
+        store_scales(0)
+        o01 = new_o(0, 1)
+        for t in range(T):
+            pass2(bank01[t], 0, 1, t, 1)
+        for t in range(T):
+            empty(o01, bank01[t], t, "s" if t % 2 == 0 else "v")
+        store_out(o01, 0, 1, 0, T)
+        o11 = new_o(1, 1)
+        for t in range(T):
+            pass2(bank11[t], 1, 1, t, 1)
+        for t in range(T):
+            empty(o11, bank11[t], t, "s" if t % 2 == 0 else "v")
+        store_out(o11, 1, 1, 0, T)
+        oq01 = weave_out(o01, "s")
+        oq11 = weave_out(o11, "v")
+        quant_out(oq01, 0, 1)
+        store_codes(0, 1)
+        quant_out(oq11, 1, 1)
+        store_codes(1, 1)
+        store_scales(1)

@@ -16,8 +16,8 @@ P = 128
 D = 1024
 T = 4
 G = 2
-H = 2
-NH = 512
+HALF = 512
+QUART = 256
 FLOPS = 2 * 2 * D * D * D
 
 
@@ -27,56 +27,49 @@ def tile_redistributedsourcesharedoperatorstep_kernel(
     nc = tc.nc
     with ExitStack() as ctx:
         keep = ctx.enter_context(tc.tile_pool(name="keep", bufs=1))
-        raw = ctx.enter_context(tc.tile_pool(name="raw", bufs=1))
-        grp = ctx.enter_context(tc.tile_pool(name="grp", bufs=3))
-        mid = ctx.enter_context(tc.tile_pool(name="mid", bufs=2))
-        res = ctx.enter_context(tc.tile_pool(name="res", bufs=2))
+        stage = ctx.enter_context(tc.tile_pool(name="stage", bufs=2))
         psum = ctx.enter_context(tc.psum_pool(name="psum", bufs=4))
         ctx.enter_context(tc.manual_schedule())
 
+        phi_sb = keep.tile([P, 8], BF16, name="phi_sb")
         eps_sb = keep.tile([P, G * T], BF16, name="eps_sb")
         kap_sb = keep.tile([P, G * T], BF16, name="kap_sb")
-        phi_sb = keep.tile([P, 8], BF16, name="phi_sb")
         nc.scalar.dma_start(out=phi_sb[:], in_=phi.rearrange("(k i) -> k i", i=8))
-        nc.scalar.dma_start(
-            out=eps_sb[:].rearrange("p (g t) -> p g t", g=G),
-            in_=eps.rearrange("(g p t) -> p g t", g=G, t=T),
-        )
-        nc.scalar.dma_start(
-            out=kap_sb[:].rearrange("p (g t) -> p g t", g=G),
-            in_=kappa.rearrange("(g p t) -> p g t", g=G, t=T),
-        )
+        for dst, src in ((eps_sb, eps), (kap_sb, kappa)):
+            nc.scalar.dma_start(
+                out=dst[:].rearrange("p (g t) -> p g t", g=G),
+                in_=src.rearrange("(g p t) -> p g t", g=G, t=T),
+            )
 
-        red_raw = raw.tile([P, 8, D], BF16, name="red_raw")
-        j_raw = raw.tile([P, G, T, D], BF16, name="j_raw")
-        lam_raw = raw.tile([P, G, T, D], BF16, name="lam_raw")
-        b_raw = raw.tile([P, G, T, D], BF16, name="b_raw")
+        red_raw = keep.tile([P, 8, D], BF16, name="red_raw")
+        j_raw = keep.tile([P, G, T, D], BF16, name="j_raw")
+        lam_raw = keep.tile([P, G, T, D], BF16, name="lam_raw")
+        b_raw = keep.tile([P, G, T, D], BF16, name="b_raw")
 
         def load_red(i):
             nc.sync.dma_start(out=red_raw[:, i, :], in_=red[P * i : P * (i + 1), :])
 
-        def load4(dst, src, g, t0, t1, c0=0, c1=D):
-            nc.sync.dma_start(
-                out=dst[:, g, t0:t1, c0:c1],
-                in_=src[512 * g : 512 * (g + 1), :].rearrange("(p t) k -> p t k", t=T)[:, t0:t1, c0:c1],
-            )
+        def load_rows(dst, src, g, t0, t1, c0=0, c1=D):
+            rows = src[HALF * g : HALF * (g + 1), :].rearrange("(p t) k -> p t k", t=T)
+            nc.sync.dma_start(out=dst[:, g, t0:t1, c0:c1], in_=rows[:, t0:t1, c0:c1])
 
-        for i in range(4):
-            load_red(i)
+        load_red(0)
+        load_red(1)
         for t in range(T):
-            load4(j_raw, j, 0, t, t + 1)
-        load4(b_raw, b, 0, 0, T, 0, NH)
-        load4(j_raw, j, 1, 0, 2)
-        load4(j_raw, j, 1, 2, 4)
-        load4(b_raw, b, 1, 0, T, 0, NH)
+            load_rows(j_raw, j, 0, t, t + 1)
+        load_red(2)
+        load_red(3)
+        load_rows(b_raw, b, 0, 0, T, 0, HALF)
+        load_rows(j_raw, j, 1, 0, 2)
+        load_rows(j_raw, j, 1, 2, 4)
+        load_rows(b_raw, b, 1, 0, T, 0, HALF)
         for i in range(4, 8):
             load_red(i)
-        load4(b_raw, b, 0, 0, T, NH, D)
-        load4(b_raw, b, 1, 0, T, NH, D)
-        load4(lam_raw, lam, 0, 0, 2)
-        load4(lam_raw, lam, 0, 2, 4)
-        load4(lam_raw, lam, 1, 0, 2)
-        load4(lam_raw, lam, 1, 2, 4)
+        load_rows(b_raw, b, 0, 0, T, HALF, D)
+        load_rows(b_raw, b, 1, 0, T, HALF, D)
+        for g in range(G):
+            load_rows(lam_raw, lam, g, 0, 2)
+            load_rows(lam_raw, lam, g, 2, 4)
 
         ident = keep.tile([P, P], F32, name="ident")
         make_identity(nc, ident[:])
@@ -91,302 +84,316 @@ def tile_redistributedsourcesharedoperatorstep_kernel(
         nc.vector.reciprocal(out=inv_col[:], in_=phi_sb[:])
         inv_phi = keep.tile([P, D], F32, name="inv_phi")
 
-        red_c = [keep.tile([P, G, NH], U32, name=f"red_c{h}", align_bytes=64) for h in range(H)]
-        red_s = [keep.tile([P, G, NH], U8, name=f"red_s{h}", align_bytes=64) for h in range(H)]
-        j_c = [keep.tile([P, T, G, P], U32, name=f"j_c{g}", align_bytes=64) for g in range(G)]
-        j_s = [keep.tile([P, T, G, P], U8, name=f"j_s{g}", align_bytes=64) for g in range(G)]
-        lam_c = [keep.tile([P, T, G, P], U32, name=f"lam_c{g}", align_bytes=64) for g in range(G)]
-        lam_s = [keep.tile([P, T, G, P], U8, name=f"lam_s{g}", align_bytes=64) for g in range(G)]
-        eta_c = [[keep.tile([P, NH], U32, name=f"eta_c{g}{h}", align_bytes=64) for h in range(H)] for g in range(G)]
-        eta_s = [[keep.tile([P, NH], U8, name=f"eta_s{g}{h}", align_bytes=64) for h in range(H)] for g in range(G)]
-        out_c = [[keep.tile([P, NH], U32, name=f"out_c{g}{h}", align_bytes=64) for h in range(H)] for g in range(G)]
-        out_s = [keep.tile([P, G, NH], U8, name=f"out_s{h}", align_bytes=64) for h in range(H)]
+        def codes(name, shape):
+            c = keep.tile([P] + shape, U32, name=name + "_c", align_bytes=64)
+            s = keep.tile([P] + shape, U8, name=name + "_s", align_bytes=64)
+            return c, s
+
+        red_q = [codes(f"red{h}", [G, HALF]) for h in range(2)]
+        j_q = [codes(f"j{g}", [T, G, P]) for g in range(G)]
+        lam_q = [codes(f"lam{g}", [T, G, P]) for g in range(G)]
+        eta_q = [codes(f"eta{g}", [D]) for g in range(G)]
+        out_c = [keep.tile([P, D], U32, name=f"out_c{g}", align_bytes=64) for g in range(G)]
+        out_s = keep.tile([P, G, D], U8, name="out_s", align_bytes=64)
+
+        def copy(eng, out, in_):
+            if eng == "s":
+                nc.scalar.copy(out=out, in_=in_)
+            else:
+                nc.vector.tensor_copy(out=out, in_=in_)
+
+        def bank(tag):
+            return psum.tile([P, HALF], F32, name="bank", tag=tag)
+
+        def group_tile(name):
+            return stage.tile([P, T * D], BF16, name=name, tag="grp", bufs=3, align_bytes=64)
 
         def turn(src, dst, eng="s"):
-            ps = psum.tile([P, G * 2, P], F32, name="turn_ps", tag="tp")
+            ps = bank("tp")
             words = src.bitcast(F32)
             for g in range(G):
                 for u in range(2):
-                    nc.tensor.transpose(ps[:, 2 * g + u, :], words[:, 256 * g + u : 256 * (g + 1) : 2], ident[:])
-            src_ps = ps[:].rearrange("p (g u) r -> p g r u", u=2)
-            if eng == "s":
-                nc.scalar.copy(out=dst, in_=src_ps)
-            else:
-                nc.vector.tensor_copy(out=dst, in_=src_ps)
+                    o = P * (2 * g + u)
+                    nc.tensor.transpose(ps[:, o : o + P], words[:, 256 * g + u : 256 * (g + 1) : 2], ident[:])
+            copy(eng, dst, ps[:].rearrange("p (g u r) -> p g r u", g=G, u=2))
 
-        def word_view(tile4096, g_outer):
-            flat = tile4096[:].bitcast(F32)
-            if g_outer:
-                return flat.rearrange("p (g n u) -> p g n u", g=G, u=2)
-            return flat.rearrange("p (t g n u) -> p t g n u", t=T, g=G, u=2)
-
-
-        def turn_red(tile, i):
-            turn(red_raw[:, i, :], word_view(tile, True)[:, :, P * (i % 4) : P * (i % 4 + 1), :])
+        def turn_red(tile, i, eng="s"):
+            dst = tile[:].bitcast(F32).rearrange("p (g n u) -> p g n u", g=G, u=2)
+            turn(red_raw[:, i, :], dst[:, :, P * (i % 4) : P * (i % 4 + 1), :], eng)
 
         def quant_red(tile, h, pair):
             src = tile[:].rearrange("p (g w) -> p g w", g=G)
+            cols = slice(QUART * pair, QUART * (pair + 1))
             for g in range(G):
                 nc.vector.quantize_mx(
-                    out=red_c[h][:, g, 256 * pair : 256 * (pair + 1)].bitcast(FP8X4),
-                    scales=red_s[h][:, g, 256 * pair : 256 * (pair + 1)],
-                    in_=src[:, g, 1024 * pair : 1024 * (pair + 1)],
+                    out=red_q[h][0][:, g, cols].bitcast(FP8X4),
+                    scales=red_q[h][1][:, g, cols],
+                    in_=src[:, g, D * pair : D * (pair + 1)],
                 )
 
-        def turn_slot(raw_tile, tile, g, t):
-            turn(raw_tile[:, g, t, :], word_view(tile, False)[:, t, :, :, :])
+        def turn_slot(raw_tile, tile, g, t, eng="s"):
+            dst = tile[:].bitcast(F32).rearrange("p (t g n u) -> p t g n u", t=T, g=G, u=2)
+            turn(raw_tile[:, g, t, :], dst[:, t, :, :, :], eng)
 
-        def quant_slot(tile, codes, scales, t0, t1):
+        def quant_slot(tile, q, t0, t1):
             nc.vector.quantize_mx(
-                out=codes[:, t0:t1].rearrange("p t g m -> p (t g m)").bitcast(FP8X4),
-                scales=scales[:, t0:t1].rearrange("p t g m -> p (t g m)"),
-                in_=tile[:, 1024 * t0 : 1024 * t1],
+                out=q[0][:, t0:t1].rearrange("p t g m -> p (t g m)").bitcast(FP8X4),
+                scales=q[1][:, t0:t1].rearrange("p t g m -> p (t g m)"),
+                in_=tile[:, D * t0 : D * t1],
             )
 
-        def stage1(r, h, t, banks):
-            ps = psum.tile([P, NH], F32, name="mm_ps", tag="mm")
+        def stage1(r, t, c0, c1):
+            ps = bank("mm")
+            h = c0 // HALF
+            cols = slice(c0 - HALF * h, c1 - HALF * h)
             for g in range(G):
                 nc.tensor.matmul_mx(
-                    out=ps[:],
-                    lhsT=j_c[r][:, t, g, :].bitcast(FP8X4),
-                    lhsT_scale=j_s[r][:, t, g, :],
-                    rhs=red_c[h][:, g, :].bitcast(FP8X4),
-                    rhs_scale=red_s[h][:, g, :],
+                    out=ps[:, : c1 - c0],
+                    lhsT=j_q[r][0][:, t, g, :].bitcast(FP8X4),
+                    lhsT_scale=j_q[r][1][:, t, g, :],
+                    rhs=red_q[h][0][:, g, cols].bitcast(FP8X4),
+                    rhs_scale=red_q[h][1][:, g, cols],
                     start=(g == 0),
                     stop=(g == G - 1),
                 )
-            banks[t] = ps
+            return ps
 
-        def scale_bank(r, h, t, banks, u):
-            k = T * r + t
+        def scatter(ps, u, r, t, c0, c1):
+            h = c0 // HALF
             nc.vector.scalar_tensor_tensor(
-                out=u[:, t, :], in0=banks[t][:], scalar=fac_a[:, k : k + 1],
-                in1=inv_phi[:, NH * h : NH * (h + 1)], op0=ALU.mult, op1=ALU.mult,
+                out=u[:, t, c0 - HALF * h : c1 - HALF * h],
+                in0=ps[:, : c1 - c0],
+                scalar=fac_a[:, T * r + t : T * r + t + 1],
+                in1=inv_phi[:, c0:c1],
+                op0=ALU.mult,
+                op1=ALU.mult,
             )
 
-        def new_w(r, h):
-            return mid.tile([P, T, NH], F32, name=f"w{r}{h}", tag="w", bufs=3)
-
-        def thermal(w, r, h, t, eng):
-            k = T * r + t
-            src = b_raw[:, r, t, NH * h : NH * (h + 1)]
+        def thermal(w, r, h, t, eng="s"):
+            factor = fac_b[:, T * r + t : T * r + t + 1]
+            src = b_raw[:, r, t, HALF * h : HALF * (h + 1)]
             if eng == "s":
-                nc.scalar.activation(out=w[:, t, :], in_=src, func=ACT.Copy, scale=fac_b[:, k : k + 1])
+                nc.scalar.activation(out=w[:, t, :], in_=src, func=ACT.Copy, scale=factor)
             else:
-                nc.vector.tensor_scalar(out=w[:, t, :], in0=src, scalar1=fac_b[:, k : k + 1], scalar2=None, op0=ALU.mult)
+                nc.vector.tensor_scalar(out=w[:, t, :], in0=src, scalar1=factor, scalar2=None, op0=ALU.mult)
 
-        def add_eta(u, w):
-            eta = mid.tile([P, NH * T], BF16, name="eta", tag="eta", align_bytes=64)
+        def add_eta(u, w, c0, c1):
+            h = c0 // HALF
+            cols = slice(c0 - HALF * h, c1 - HALF * h)
+            eta = stage.tile([P, HALF * T], BF16, name="eta", tag="eta", align_bytes=64)
             nc.vector.tensor_tensor(
-                out=eta[:].rearrange("p (c i t) -> p c t i", i=4, t=T),
-                in0=u[:].rearrange("p t (c i) -> p c t i", i=4),
-                in1=w[:].rearrange("p t (c i) -> p c t i", i=4),
+                out=eta[:, : T * (c1 - c0)].rearrange("p (c i t) -> p c t i", i=4, t=T),
+                in0=u[:, :, cols].rearrange("p t (c i) -> p c t i", i=4),
+                in1=w[:, :, cols].rearrange("p t (c i) -> p c t i", i=4),
                 op=ALU.add,
             )
             return eta
 
-        def quant_eta(eta, r, h):
-            nc.vector.quantize_mx(out=eta_c[r][h][:].bitcast(FP8X4), scales=eta_s[r][h][:], in_=eta[:])
+        def quant_eta(eta, r, c0, c1):
+            nc.vector.quantize_mx(
+                out=eta_q[r][0][:, c0:c1].bitcast(FP8X4),
+                scales=eta_q[r][1][:, c0:c1],
+                in_=eta[:, : T * (c1 - c0)],
+            )
 
-        def pass2(ps, q, h, t, r):
+        def pass2(ps, q, t, r, c0, c1):
             nc.tensor.matmul_mx(
-                out=ps[:],
-                lhsT=lam_c[q][:, t, r, :].bitcast(FP8X4),
-                lhsT_scale=lam_s[q][:, t, r, :],
-                rhs=eta_c[r][h][:].bitcast(FP8X4),
-                rhs_scale=eta_s[r][h][:],
+                out=ps[:, : c1 - c0],
+                lhsT=lam_q[q][0][:, t, r, :].bitcast(FP8X4),
+                lhsT_scale=lam_q[q][1][:, t, r, :],
+                rhs=eta_q[r][0][:, c0:c1].bitcast(FP8X4),
+                rhs_scale=eta_q[r][1][:, c0:c1],
                 start=(r == 0),
                 stop=(r == G - 1),
             )
 
-        def empty(o, ps, t, eng):
-            if eng == "s":
-                nc.scalar.copy(out=o[:, t, :], in_=ps[:])
-            else:
-                nc.vector.tensor_copy(out=o[:, t, :], in_=ps[:])
+        def new_o():
+            return stage.tile([P, T, HALF], F32, name="o", tag="o", bufs=4)
 
-        def store_out(o, q, h, t0, t1):
-            nc.sync.dma_start(
-                out=out_0[512 * q : 512 * (q + 1), :].rearrange("(p t) n -> p t n", t=T)[:, t0:t1, NH * h : NH * (h + 1)],
-                in_=o[:, t0:t1, :],
-            )
+        def empty(o, ps, t, c0, c1, eng="s"):
+            copy(eng, o[:, t, c0 % HALF : c0 % HALF + c1 - c0], ps[:, : c1 - c0])
 
-        def weave_out(o, eng):
-            oq = res.tile([P, NH * T], BF16, name="oq", tag="oq", align_bytes=64)
-            dst = oq[:].rearrange("p (c i t) -> p c t i", i=4, t=T)
-            src = o[:].rearrange("p t (c i) -> p c t i", i=4)
-            if eng == "s":
-                nc.scalar.copy(out=dst, in_=src)
-            else:
-                nc.vector.tensor_copy(out=dst, in_=src)
+        def store_out(o, q, t0, t1, c0, c1):
+            rows = out_0[HALF * q : HALF * (q + 1), :].rearrange("(p t) n -> p t n", t=T)
+            nc.sync.dma_start(out=rows[:, t0:t1, c0:c1], in_=o[:, t0:t1, c0 % HALF : c0 % HALF + c1 - c0])
+
+        def weave(o, c0, c1, eng):
+            n = c1 - c0
+            oq = stage.tile([P, HALF * T], BF16, name="oq", tag="oq", bufs=4, align_bytes=64)
+            copy(eng, oq[:, : T * n].rearrange("p (c i t) -> p c t i", i=4, t=T),
+                 o[:, :, c0 % HALF : c0 % HALF + n].rearrange("p t (c i) -> p c t i", i=4))
             return oq
 
-        def quant_out(oq, q, h):
-            nc.vector.quantize_mx(out=out_c[q][h][:].bitcast(FP8X4), scales=out_s[h][:, q, :], in_=oq[:])
-
-        def store_codes(q, h):
-            nc.sync.dma_start(
-                out=out_1[q].rearrange("p m t -> p (m t)").bitcast(I32)[:, NH * h : NH * (h + 1)],
-                in_=out_c[q][h][:].bitcast(I32),
+        def quant_out(oq, q, c0, c1):
+            nc.vector.quantize_mx(
+                out=out_c[q][:, c0:c1].bitcast(FP8X4), scales=out_s[:, q, c0:c1], in_=oq[:, : T * (c1 - c0)]
             )
 
-        def store_scales(h):
+        def store_codes(q, c0, c1):
+            nc.sync.dma_start(
+                out=out_1[q].rearrange("p m t -> p (m t)").bitcast(I32)[:, c0:c1],
+                in_=out_c[q][:, c0:c1].bitcast(I32),
+            )
+
+        def store_scales(c0, c1):
             for quad in range(4):
                 nc.sync.dma_start(
-                    out=out_2[:, 4 * quad : 4 * quad + 4, NH * h : NH * (h + 1)].rearrange("g q n -> q g n").bitcast(I32),
-                    in_=out_s[h][32 * quad : 32 * quad + 4, :, :].bitcast(I32),
+                    out=out_2[:, 4 * quad : 4 * quad + 4, c0:c1].rearrange("g q n -> q g n").bitcast(I32),
+                    in_=out_s[32 * quad : 32 * quad + 4, :, c0:c1].bitcast(I32),
                 )
 
-        def group_tile(name):
-            return grp.tile([P, T * D], BF16, name=name, tag="grp", align_bytes=64)
+        def new_u():
+            return stage.tile([P, T, HALF], F32, name="u", tag="u", bufs=2)
 
-        def new_u(r, h):
-            return mid.tile([P, T, NH], F32, name=f"u{r}{h}", tag="u")
+        def new_w():
+            return stage.tile([P, T, HALF], F32, name="w", tag="w", bufs=2)
 
-        def new_o(q, h):
-            return res.tile([P, T, NH], F32, name=f"o{q}{h}", tag="o", bufs=3)
+        C2 = HALF + QUART
 
-        def new_bank(tag):
-            return psum.tile([P, NH], F32, name="out_ps", tag=tag)
-
-        def turn4(raw_tile, tile, g):
-            for t in range(T):
-                turn_slot(raw_tile, tile, g, t)
-
-        for half in range(2):
-            ps = psum.tile([P, 4, P], F32, name="phi_ps", tag="mm")
+        def phi_rows(half, eng):
+            ps = bank("mm")
             for i in range(4):
                 k = 4 * half + i
-                nc.tensor.transpose(ps[:, i, :], inv_col[:, k : k + 1].to_broadcast([P, P]), ident[:])
-            nc.vector.tensor_copy(
-                out=inv_phi[:].rearrange("p (k i) -> p k i", i=8)[:, :, 4 * half : 4 * half + 4],
-                in_=ps[:].rearrange("p i k -> p k i"),
-            )
+                nc.tensor.transpose(ps[:, P * i : P * (i + 1)], inv_col[:, k : k + 1].to_broadcast([P, P]), ident[:])
+            copy(eng, inv_phi[:].rearrange("p (k i) -> p k i", i=8)[:, :, 4 * half : 4 * half + 4],
+                ps[:].rearrange("p (i k) -> p k i", i=4))
+
+        phi_rows(0, "s")
+        phi_rows(1, "v")
         gr0 = group_tile("gr0")
-        turn_red(gr0, 0)
-        turn_red(gr0, 1)
-        quant_red(gr0, 0, 0)
-        turn_red(gr0, 2)
-        turn_red(gr0, 3)
-        quant_red(gr0, 0, 1)
         gj0 = group_tile("gj0")
-        u00 = new_u(0, 0)
-        w00 = new_w(0, 0)
+        u00 = new_u()
+        w00 = new_w()
         banks = {}
-        for t in range(4):
-            turn_slot(j_raw, gj0, 0, t)
-            quant_slot(gj0, j_c[0], j_s[0], t, t + 1)
-        for t in range(4):
-            stage1(0, 0, t, banks)
+        turn_red(gr0, 0, "s")
+        turn_red(gr0, 1, "v")
+        quant_red(gr0, 0, 0)
         for t in range(T):
-            thermal(w00, 0, 0, t, "s" if t < 2 else "v")
-            scale_bank(0, 0, t, banks, u00)
+            turn_slot(j_raw, gj0, 0, t, "s" if t != 1 else "v")
+        turn_red(gr0, 2, "s")
+        for t in range(T):
+            quant_slot(gj0, j_q[0], t, t + 1)
+        for t in range(T):
+            banks[t] = stage1(0, t, 0, QUART)
+            if t == 0:
+                turn_red(gr0, 3, "s")
         gj1 = group_tile("gj1")
-        turn4(j_raw, gj1, 1)
-        quant_slot(gj1, j_c[1], j_s[1], 0, 2)
-        eta00 = add_eta(u00, w00)
-        quant_slot(gj1, j_c[1], j_s[1], 2, 4)
-        banks = {}
-        u10 = new_u(1, 0)
-        w10 = new_w(1, 0)
         for t in range(T):
-            thermal(w10, 1, 0, t, "s")
+            scatter(banks[t], u00, 0, t, 0, QUART)
+            if t == 1:
+                quant_red(gr0, 0, 1)
+        thermal(w00, 0, 0, 0)
+        turn_slot(j_raw, gj1, 1, 0)
+        turn_slot(j_raw, gj1, 1, 1)
+        thermal(w00, 0, 0, 1)
+        for t in range(T):
+            banks[t] = stage1(0, t, QUART, HALF)
+        turn_slot(j_raw, gj1, 1, 2)
+        turn_slot(j_raw, gj1, 1, 3)
+        for t in range(T):
+            scatter(banks[t], u00, 0, t, QUART, HALF)
+        for t in range(2, T):
+            thermal(w00, 0, 0, t)
         gr1 = group_tile("gr1")
-        for i in range(4):
-            turn_red(gr1, 4 + i)
+        u10 = new_u()
+        w10 = new_w()
+        quant_slot(gj1, j_q[1], 0, 2)
+        turn_red(gr1, 4)
+        turn_red(gr1, 5)
+        turn_red(gr1, 6)
+        turn_red(gr1, 7)
+        quant_slot(gj1, j_q[1], 2, 4)
         for t in range(T):
-            stage1(1, 0, t, banks)
-        scale_bank(1, 0, 0, banks, u10)
-        scale_bank(1, 0, 1, banks, u10)
-        quant_eta(eta00, 0, 0)
-        scale_bank(1, 0, 2, banks, u10)
-        scale_bank(1, 0, 3, banks, u10)
+            banks[t] = stage1(1, t, 0, HALF)
+        eta00 = add_eta(u00, w00, 0, HALF)
+        for t in range(T):
+            thermal(w10, 1, 0, t)
+        for t in range(T):
+            scatter(banks[t], u10, 1, t, 0, HALF)
+            if t == 1:
+                quant_eta(eta00, 0, 0, HALF)
         quant_red(gr1, 1, 0)
         quant_red(gr1, 1, 1)
-        eta10 = add_eta(u10, w10)
-        u01 = new_u(0, 1)
-        w01 = new_w(0, 1)
-        for t in range(T):
-            thermal(w01, 0, 1, t, "s")
         gl0 = group_tile("gl0")
-        turn4(lam_raw, gl0, 0)
-        banks = {}
         for t in range(T):
-            stage1(0, 1, t, banks)
-        scale_bank(0, 1, 0, banks, u01)
-        scale_bank(0, 1, 1, banks, u01)
-        quant_eta(eta10, 1, 0)
-        scale_bank(0, 1, 2, banks, u01)
-        scale_bank(0, 1, 3, banks, u01)
-        quant_slot(gl0, lam_c[0], lam_s[0], 0, 2)
-        eta01 = add_eta(u01, w01)
-        quant_slot(gl0, lam_c[0], lam_s[0], 2, 4)
-        banks = {}
-        u11 = new_u(1, 1)
-        w11 = new_w(1, 1)
+            turn_slot(lam_raw, gl0, 0, t)
+        u01 = new_u()
+        w01 = new_w()
         gl1 = group_tile("gl1")
-        turn4(lam_raw, gl1, 1)
         for t in range(T):
-            stage1(1, 1, t, banks)
+            banks[t] = stage1(0, t, HALF, D)
+        eta10 = add_eta(u10, w10, 0, HALF)
+        quant_slot(gl0, lam_q[0], 0, 2)
+        quant_slot(gl0, lam_q[0], 2, 4)
         for t in range(T):
-            thermal(w11, 1, 1, t, "s")
-        scale_bank(1, 1, 0, banks, u11)
-        scale_bank(1, 1, 1, banks, u11)
-        quant_eta(eta01, 0, 1)
-        scale_bank(1, 1, 2, banks, u11)
-        scale_bank(1, 1, 3, banks, u11)
-        quant_slot(gl1, lam_c[1], lam_s[1], 0, 2)
-        quant_slot(gl1, lam_c[1], lam_s[1], 2, 4)
-        eta11 = add_eta(u11, w11)
-
-        o00 = new_o(0, 0)
+            thermal(w01, 0, 1, t)
         for t in range(T):
-            ps = new_bank("tp")
-            pass2(ps, 0, 0, t, 0)
-            pass2(ps, 0, 0, t, 1)
-            empty(o00, ps, t, "s")
-        store_out(o00, 0, 0, 0, T)
-        o10 = new_o(1, 0)
+            turn_slot(lam_raw, gl1, 1, t)
         for t in range(T):
-            ps = new_bank("tp")
-            pass2(ps, 1, 0, t, 0)
-            pass2(ps, 1, 0, t, 1)
-            empty(o10, ps, t, "s")
-        store_out(o10, 1, 0, 0, T)
-        oq00 = weave_out(o00, "s")
-        quant_eta(eta11, 1, 1)
-        bank01 = []
+            scatter(banks[t], u01, 0, t, HALF, D)
+            if t == 1:
+                quant_eta(eta10, 1, 0, HALF)
+        u11 = new_u()
+        w11 = new_w()
         for t in range(T):
-            ps = new_bank("mm")
-            pass2(ps, 0, 1, t, 0)
-            bank01.append(ps)
-        bank11 = []
+            banks[t] = stage1(1, t, HALF, C2)
         for t in range(T):
-            ps = new_bank("tp")
-            pass2(ps, 1, 1, t, 0)
-            bank11.append(ps)
-        oq10 = weave_out(o10, "v")
-        quant_out(oq00, 0, 0)
-        store_codes(0, 0)
-        quant_out(oq10, 1, 0)
-        store_codes(1, 0)
-        store_scales(0)
-        o01 = new_o(0, 1)
+            thermal(w11, 1, 1, t)
+        quant_slot(gl1, lam_q[1], 0, 2)
+        quant_slot(gl1, lam_q[1], 2, 4)
+        eta01 = add_eta(u01, w01, HALF, D)
+        o0 = [new_o(), new_o()]
+        for q in range(2):
+            for t in range(T):
+                ps = bank("tp")
+                pass2(ps, q, t, 0, 0, HALF)
+                pass2(ps, q, t, 1, 0, HALF)
+                empty(o0[q], ps, t, 0, HALF)
+            store_out(o0[q], q, 0, T, 0, HALF)
+        oq00 = weave(o0[0], 0, HALF, "s")
+        oq10 = weave(o0[1], 0, HALF, "s")
         for t in range(T):
-            pass2(bank01[t], 0, 1, t, 1)
+            scatter(banks[t], u11, 1, t, HALF, C2)
+            if t == 1:
+                quant_eta(eta01, 0, HALF, D)
         for t in range(T):
-            empty(o01, bank01[t], t, "s" if t % 2 == 0 else "v")
-        store_out(o01, 0, 1, 0, T)
-        o11 = new_o(1, 1)
+            banks[t] = stage1(1, t, C2, D)
+        eta11 = add_eta(u11, w11, HALF, C2)
         for t in range(T):
-            pass2(bank11[t], 1, 1, t, 1)
-        for t in range(T):
-            empty(o11, bank11[t], t, "s" if t % 2 == 0 else "v")
-        store_out(o11, 1, 1, 0, T)
-        oq01 = weave_out(o01, "s")
-        oq11 = weave_out(o11, "v")
-        quant_out(oq01, 0, 1)
-        store_codes(0, 1)
-        quant_out(oq11, 1, 1)
-        store_codes(1, 1)
-        store_scales(1)
+            scatter(banks[t], u11, 1, t, C2, D)
+            if t == 1:
+                quant_eta(eta11, 1, HALF, C2)
+        eta11b = add_eta(u11, w11, C2, D)
+        quant_out(oq00, 0, 0, HALF)
+        store_codes(0, 0, HALF)
+        quant_eta(eta11b, 1, C2, D)
+        o1 = [new_o(), new_o()]
+        oq1 = {}
+        for q in range(2):
+            for t in range(T):
+                ps = bank("mm" if q == 0 else "tp")
+                pass2(ps, q, t, 0, HALF, C2)
+                pass2(ps, q, t, 1, HALF, C2)
+                empty(o1[q], ps, t, HALF, C2, "s")
+            store_out(o1[q], q, 0, T, HALF, C2)
+        oq1[0, 0] = weave(o1[0], HALF, C2, "v")
+        quant_out(oq10, 1, 0, HALF)
+        store_codes(1, 0, HALF)
+        store_scales(0, HALF)
+        oq1[1, 0] = weave(o1[1], HALF, C2, "s")
+        quant_out(oq1[0, 0], 0, HALF, C2)
+        for q in range(2):
+            for t in range(T):
+                ps = bank("mm" if q == 0 else "tp")
+                pass2(ps, q, t, 0, C2, D)
+                pass2(ps, q, t, 1, C2, D)
+                empty(o1[q], ps, t, C2, D, "s" if q == 0 else "v")
+            store_out(o1[q], q, 0, T, C2, D)
+        quant_out(oq1[1, 0], 1, HALF, C2)
+        oq1[0, 1] = weave(o1[0], C2, D, "s")
+        oq1[1, 1] = weave(o1[1], C2, D, "v")
+        quant_out(oq1[1, 1], 1, C2, D)
+        store_codes(1, HALF, D)
+        quant_out(oq1[0, 1], 0, C2, D)
+        store_codes(0, HALF, D)
+        store_scales(HALF, D)

@@ -41,38 +41,45 @@ def tile_redistributedsourcesharedoperatorstep_kernel(
                 in_=src.rearrange("(g p t) -> p g t", g=G, t=T),
             )
 
-        red_raw = keep.tile([P, 8, D], BF16, name="red_raw")
-        j_raw = keep.tile([P, G, T, D], BF16, name="j_raw")
-        lam_raw = keep.tile([P, G, T, D], BF16, name="lam_raw")
-        b_raw = keep.tile([P, G, T, D], BF16, name="b_raw")
+        red_raw = [stage.tile([P, T, D], BF16, name=f"red_raw{h}", tag="rows", bufs=8) for h in range(2)]
+        j_raw = [stage.tile([P, T, D], BF16, name=f"j_raw{g}", tag="rows", bufs=8) for g in range(G)]
+        lam_raw = [stage.tile([P, T, D], BF16, name=f"lam_raw{g}", tag="rows", bufs=8) for g in range(G)]
+        b_raw = [stage.tile([P, T, D], BF16, name=f"b_raw{g}", tag="rows", bufs=8) for g in range(G)]
 
         def load_red(i):
-            nc.sync.dma_start(out=red_raw[:, i, :], in_=red[P * i : P * (i + 1), :])
+            nc.sync.dma_start(out=red_raw[i // T][:, i % T, :], in_=red[P * i : P * (i + 1), :])
 
         def load_rows(dst, src, g, t0, t1, c0=0, c1=D):
             rows = src[HALF * g : HALF * (g + 1), :].rearrange("(p t) k -> p t k", t=T)
-            nc.sync.dma_start(out=dst[:, g, t0:t1, c0:c1], in_=rows[:, t0:t1, c0:c1])
+            nc.sync.dma_start(out=dst[g][:, t0:t1, c0:c1], in_=rows[:, t0:t1, c0:c1])
 
+        load_rows(j_raw, j, 0, 0, 1)
         load_red(0)
+        load_rows(j_raw, j, 0, 1, 2)
         load_red(1)
-        for t in range(T):
-            load_rows(j_raw, j, 0, t, t + 1)
+        load_rows(j_raw, j, 0, 2, 3)
         load_red(2)
-        load_red(3)
-        load_rows(b_raw, b, 0, 0, T, 0, HALF)
         load_rows(j_raw, j, 1, 0, 2)
+        load_red(3)
+        load_rows(j_raw, j, 0, 3, 4)
+        load_rows(b_raw, b, 0, 0, T, 0, HALF)
         load_rows(j_raw, j, 1, 2, 4)
         load_rows(b_raw, b, 1, 0, T, 0, HALF)
-        for i in range(4, 8):
-            load_red(i)
         load_rows(b_raw, b, 0, 0, T, HALF, D)
+        load_red(4)
+        load_rows(lam_raw, lam, 1, 0, 2)
+        load_red(5)
+        load_rows(lam_raw, lam, 1, 2, 4)
+        load_rows(lam_raw, lam, 0, 0, 2)
+        load_red(6)
+        load_red(7)
         load_rows(b_raw, b, 1, 0, T, HALF, D)
-        for g in range(G):
-            load_rows(lam_raw, lam, g, 0, 2)
-            load_rows(lam_raw, lam, g, 2, 4)
+        load_rows(lam_raw, lam, 0, 2, 4)
 
         ident = keep.tile([P, P], F32, name="ident")
         make_identity(nc, ident[:])
+        ident_bf = keep.tile([P, P], BF16, name="ident_bf")
+        nc.vector.tensor_copy(out=ident_bf[:], in_=ident[:])
 
         fac_a = keep.tile([P, G * T], F32, name="fac_a")
         fac_b = keep.tile([P, G * T], F32, name="fac_b")
@@ -80,8 +87,6 @@ def tile_redistributedsourcesharedoperatorstep_kernel(
         nc.gpsimd.tensor_scalar(out=one_m[:], in0=eps_sb[:], scalar1=-1.0, scalar2=1.0, op0=ALU.mult, op1=ALU.add)
         nc.gpsimd.tensor_tensor(out=fac_a[:], in0=kap_sb[:], in1=one_m[:], op=ALU.mult)
         nc.gpsimd.tensor_tensor(out=fac_b[:], in0=kap_sb[:], in1=eps_sb[:], op=ALU.mult)
-        inv_col = keep.tile([P, 8], F32, name="inv_col")
-        nc.vector.reciprocal(out=inv_col[:], in_=phi_sb[:])
         inv_phi = keep.tile([P, D], F32, name="inv_phi")
 
         def codes(name, shape):
@@ -90,8 +95,10 @@ def tile_redistributedsourcesharedoperatorstep_kernel(
             return c, s
 
         red_q = [codes(f"red{h}", [G, HALF]) for h in range(2)]
-        j_q = [codes(f"j{g}", [T, G, P]) for g in range(G)]
-        lam_q = [codes(f"lam{g}", [T, G, P]) for g in range(G)]
+        row_q = {}
+        for m in "jl":
+            for g in range(G):
+                row_q[m, g] = codes(f"{m}{g}", [T, G, P])
         eta_q = [codes(f"eta{g}", [D]) for g in range(G)]
         out_c = [keep.tile([P, D], U32, name=f"out_c{g}", align_bytes=64) for g in range(G)]
         out_s = keep.tile([P, G, D], U8, name="out_s", align_bytes=64)
@@ -102,131 +109,171 @@ def tile_redistributedsourcesharedoperatorstep_kernel(
             else:
                 nc.vector.tensor_copy(out=out, in_=in_)
 
-        def bank(tag):
-            return psum.tile([P, HALF], F32, name="bank", tag=tag)
+        banks = {}
+        tiles = {}
 
-        def group_tile(name):
-            return stage.tile([P, T * D], BF16, name=name, tag="grp", bufs=3, align_bytes=64)
+        def bank(key, tag):
+            banks[key] = psum.tile([P, HALF], F32, name="bank", tag=tag)
+            return banks[key]
 
-        def turn(src, dst, eng="s"):
-            ps = bank("tp")
+        def tile_of(kind, key, shape, dtype, bufs, align=None):
+            if (kind, key) not in tiles:
+                tiles[kind, key] = stage.tile([P] + shape, dtype, name=kind, tag=kind, bufs=bufs, align_bytes=align)
+            return tiles[kind, key]
+
+        def grouped(key):
+            return tile_of("grp", key, [T * D], BF16, 4, 64)
+
+        def phi_rows():
+            ps = psum.tile([P, D], BF16, name="phi_ps", tag="mm")
+            for i in range(8):
+                nc.tensor.transpose(ps[:, P * i : P * (i + 1)], phi_sb[:, i : i + 1].to_broadcast([P, P]), ident_bf[:])
+            banks["phi"] = ps
+
+        def phi_inv():
+            nc.vector.reciprocal(
+                out=inv_phi[:].rearrange("p (k i) -> p k i", i=8),
+                in_=banks["phi"][:].rearrange("p (i k) -> p k i", i=8),
+            )
+
+        def turn(key, src):
+            ps = bank(key, "tp")
             words = src.bitcast(F32)
             for g in range(G):
                 for u in range(2):
                     o = P * (2 * g + u)
                     nc.tensor.transpose(ps[:, o : o + P], words[:, 256 * g + u : 256 * (g + 1) : 2], ident[:])
-            copy(eng, dst, ps[:].rearrange("p (g u r) -> p g r u", g=G, u=2))
 
-        def turn_red(tile, i, eng="s"):
-            dst = tile[:].bitcast(F32).rearrange("p (g n u) -> p g n u", g=G, u=2)
-            turn(red_raw[:, i, :], dst[:, :, P * (i % 4) : P * (i % 4 + 1), :], eng)
+        def lay(key, dst, eng):
+            copy(eng, dst, banks[key][:].rearrange("p (g u r) -> p g r u", g=G, u=2))
 
-        def quant_red(tile, h, pair):
-            src = tile[:].rearrange("p (g w) -> p g w", g=G)
-            cols = slice(QUART * pair, QUART * (pair + 1))
+        def turn_red(i):
+            turn(("r", i), red_raw[i // T][:, i % T, :])
+
+        def lay_red(i, eng):
+            dst = grouped(("r", i // T))[:].bitcast(F32).rearrange("p (g n u) -> p g n u", g=G, u=2)
+            lay(("r", i), dst[:, :, P * (i % T) : P * (i % T + 1), :], eng)
+
+        def quant_red(pair):
+            h = pair // 2
+            src = grouped(("r", h))[:].rearrange("p (g w) -> p g w", g=G)
+            c0 = QUART * (pair % 2)
             for g in range(G):
                 nc.vector.quantize_mx(
-                    out=red_q[h][0][:, g, cols].bitcast(FP8X4),
-                    scales=red_q[h][1][:, g, cols],
-                    in_=src[:, g, D * pair : D * (pair + 1)],
+                    out=red_q[h][0][:, g, c0 : c0 + QUART].bitcast(FP8X4),
+                    scales=red_q[h][1][:, g, c0 : c0 + QUART],
+                    in_=src[:, g, T * c0 : T * (c0 + QUART)],
                 )
 
-        def turn_slot(raw_tile, tile, g, t, eng="s"):
-            dst = tile[:].bitcast(F32).rearrange("p (t g n u) -> p t g n u", t=T, g=G, u=2)
-            turn(raw_tile[:, g, t, :], dst[:, t, :, :, :], eng)
+        def turn_row(m, g, t):
+            turn((m, g, t), (j_raw if m == "j" else lam_raw)[g][:, t, :])
 
-        def quant_slot(tile, q, t0, t1):
+        def lay_row(m, g, t, eng):
+            dst = grouped((m, g))[:].bitcast(F32).rearrange("p (t g n u) -> p t g n u", t=T, g=G, u=2)
+            lay((m, g, t), dst[:, t, :, :, :], eng)
+
+        def quant_row(m, g, t0, t1):
+            q = row_q[m, g]
             nc.vector.quantize_mx(
                 out=q[0][:, t0:t1].rearrange("p t g m -> p (t g m)").bitcast(FP8X4),
                 scales=q[1][:, t0:t1].rearrange("p t g m -> p (t g m)"),
-                in_=tile[:, D * t0 : D * t1],
+                in_=grouped((m, g))[:, D * t0 : D * t1],
             )
 
-        def stage1(r, t, c0, c1):
-            ps = bank("mm")
+        def first(r, t, c0, c1):
+            ps = bank(("m", r, t, c0), "mm")
             h = c0 // HALF
             cols = slice(c0 - HALF * h, c1 - HALF * h)
+            q = row_q["j", r]
             for g in range(G):
                 nc.tensor.matmul_mx(
                     out=ps[:, : c1 - c0],
-                    lhsT=j_q[r][0][:, t, g, :].bitcast(FP8X4),
-                    lhsT_scale=j_q[r][1][:, t, g, :],
+                    lhsT=q[0][:, t, g, :].bitcast(FP8X4),
+                    lhsT_scale=q[1][:, t, g, :],
                     rhs=red_q[h][0][:, g, cols].bitcast(FP8X4),
                     rhs_scale=red_q[h][1][:, g, cols],
                     start=(g == 0),
                     stop=(g == G - 1),
                 )
-            return ps
 
-        def scatter(ps, u, r, t, c0, c1):
+        def scatter(r, t, c0, c1):
             h = c0 // HALF
+            u = tile_of("u", (r, h), [T, HALF], F32, 3)
             nc.vector.scalar_tensor_tensor(
                 out=u[:, t, c0 - HALF * h : c1 - HALF * h],
-                in0=ps[:, : c1 - c0],
+                in0=banks["m", r, t, c0][:, : c1 - c0],
                 scalar=fac_a[:, T * r + t : T * r + t + 1],
                 in1=inv_phi[:, c0:c1],
                 op0=ALU.mult,
                 op1=ALU.mult,
             )
 
-        def thermal(w, r, h, t, eng="s"):
+        def thermal(r, h, t, eng):
+            w = tile_of("w", (r, h), [T, HALF], F32, 3)
             factor = fac_b[:, T * r + t : T * r + t + 1]
-            src = b_raw[:, r, t, HALF * h : HALF * (h + 1)]
+            src = b_raw[r][:, t, HALF * h : HALF * (h + 1)]
             if eng == "s":
                 nc.scalar.activation(out=w[:, t, :], in_=src, func=ACT.Copy, scale=factor)
             else:
                 nc.vector.tensor_scalar(out=w[:, t, :], in0=src, scalar1=factor, scalar2=None, op0=ALU.mult)
 
-        def add_eta(u, w, c0, c1):
+        def add_eta(r, c0, c1):
             h = c0 // HALF
             cols = slice(c0 - HALF * h, c1 - HALF * h)
-            eta = stage.tile([P, HALF * T], BF16, name="eta", tag="eta", align_bytes=64)
+            eta = tile_of("eta", (r, c0), [HALF * T], BF16, 2, 64)
             nc.vector.tensor_tensor(
                 out=eta[:, : T * (c1 - c0)].rearrange("p (c i t) -> p c t i", i=4, t=T),
-                in0=u[:, :, cols].rearrange("p t (c i) -> p c t i", i=4),
-                in1=w[:, :, cols].rearrange("p t (c i) -> p c t i", i=4),
+                in0=tiles["u", (r, h)][:, :, cols].rearrange("p t (c i) -> p c t i", i=4),
+                in1=tiles["w", (r, h)][:, :, cols].rearrange("p t (c i) -> p c t i", i=4),
                 op=ALU.add,
             )
-            return eta
 
-        def quant_eta(eta, r, c0, c1):
+        def quant_eta(r, c0, c1):
             nc.vector.quantize_mx(
                 out=eta_q[r][0][:, c0:c1].bitcast(FP8X4),
                 scales=eta_q[r][1][:, c0:c1],
-                in_=eta[:, : T * (c1 - c0)],
+                in_=tiles["eta", (r, c0)][:, : T * (c1 - c0)],
             )
 
-        def pass2(ps, q, t, r, c0, c1):
-            nc.tensor.matmul_mx(
-                out=ps[:, : c1 - c0],
-                lhsT=lam_q[q][0][:, t, r, :].bitcast(FP8X4),
-                lhsT_scale=lam_q[q][1][:, t, r, :],
-                rhs=eta_q[r][0][:, c0:c1].bitcast(FP8X4),
-                rhs_scale=eta_q[r][1][:, c0:c1],
-                start=(r == 0),
-                stop=(r == G - 1),
-            )
+        def second(q, t, c0, c1, tag):
+            ps = bank(("p", q, t, c0), tag)
+            lam8 = row_q["l", q]
+            for r in range(G):
+                nc.tensor.matmul_mx(
+                    out=ps[:, : c1 - c0],
+                    lhsT=lam8[0][:, t, r, :].bitcast(FP8X4),
+                    lhsT_scale=lam8[1][:, t, r, :],
+                    rhs=eta_q[r][0][:, c0:c1].bitcast(FP8X4),
+                    rhs_scale=eta_q[r][1][:, c0:c1],
+                    start=(r == 0),
+                    stop=(r == G - 1),
+                )
 
-        def new_o():
-            return stage.tile([P, T, HALF], F32, name="o", tag="o", bufs=4)
+        def result(q, c0):
+            return tile_of("rows", (q, c0 // HALF), [T, HALF], F32, 8)
 
-        def empty(o, ps, t, c0, c1, eng="s"):
-            copy(eng, o[:, t, c0 % HALF : c0 % HALF + c1 - c0], ps[:, : c1 - c0])
+        def empty(q, t, c0, c1, eng):
+            o = result(q, c0)
+            copy(eng, o[:, t, c0 % HALF : c0 % HALF + c1 - c0], banks["p", q, t, c0][:, : c1 - c0])
 
-        def store_out(o, q, t0, t1, c0, c1):
+        def store_out(q, t0, t1, c0, c1):
             rows = out_0[HALF * q : HALF * (q + 1), :].rearrange("(p t) n -> p t n", t=T)
-            nc.sync.dma_start(out=rows[:, t0:t1, c0:c1], in_=o[:, t0:t1, c0 % HALF : c0 % HALF + c1 - c0])
+            nc.sync.dma_start(out=rows[:, t0:t1, c0:c1], in_=result(q, c0)[:, t0:t1, c0 % HALF : c0 % HALF + c1 - c0])
 
-        def weave(o, c0, c1, eng):
+        def weave(q, c0, c1, eng):
             n = c1 - c0
-            oq = stage.tile([P, HALF * T], BF16, name="oq", tag="oq", bufs=4, align_bytes=64)
-            copy(eng, oq[:, : T * n].rearrange("p (c i t) -> p c t i", i=4, t=T),
-                 o[:, :, c0 % HALF : c0 % HALF + n].rearrange("p t (c i) -> p c t i", i=4))
-            return oq
+            oq = tile_of("oq", (q, c0), [HALF * T], BF16, 4, 64)
+            copy(
+                eng,
+                oq[:, : T * n].rearrange("p (c i t) -> p c t i", i=4, t=T),
+                result(q, c0)[:, :, c0 % HALF : c0 % HALF + n].rearrange("p t (c i) -> p c t i", i=4),
+            )
 
-        def quant_out(oq, q, c0, c1):
+        def quant_out(q, c0, c1):
             nc.vector.quantize_mx(
-                out=out_c[q][:, c0:c1].bitcast(FP8X4), scales=out_s[:, q, c0:c1], in_=oq[:, : T * (c1 - c0)]
+                out=out_c[q][:, c0:c1].bitcast(FP8X4),
+                scales=out_s[:, q, c0:c1],
+                in_=tiles["oq", (q, c0)][:, : T * (c1 - c0)],
             )
 
         def store_codes(q, c0, c1):
@@ -242,158 +289,218 @@ def tile_redistributedsourcesharedoperatorstep_kernel(
                     in_=out_s[32 * quad : 32 * quad + 4, :, c0:c1].bitcast(I32),
                 )
 
-        def new_u():
-            return stage.tile([P, T, HALF], F32, name="u", tag="u", bufs=2)
-
-        def new_w():
-            return stage.tile([P, T, HALF], F32, name="w", tag="w", bufs=2)
-
-        C2 = HALF + QUART
-
-        def phi_rows(half, eng):
-            ps = bank("mm")
-            for i in range(4):
-                k = 4 * half + i
-                nc.tensor.transpose(ps[:, P * i : P * (i + 1)], inv_col[:, k : k + 1].to_broadcast([P, P]), ident[:])
-            copy(eng, inv_phi[:].rearrange("p (k i) -> p k i", i=8)[:, :, 4 * half : 4 * half + 4],
-                ps[:].rearrange("p (i k) -> p k i", i=4))
-
-        phi_rows(0, "s")
-        phi_rows(1, "v")
-        gr0 = group_tile("gr0")
-        gj0 = group_tile("gj0")
-        u00 = new_u()
-        w00 = new_w()
-        banks = {}
-        turn_red(gr0, 0, "s")
-        turn_red(gr0, 1, "v")
-        quant_red(gr0, 0, 0)
-        for t in range(T):
-            turn_slot(j_raw, gj0, 0, t, "s" if t != 1 else "v")
-        turn_red(gr0, 2, "s")
-        for t in range(T):
-            quant_slot(gj0, j_q[0], t, t + 1)
-        for t in range(T):
-            banks[t] = stage1(0, t, 0, QUART)
-            if t == 0:
-                turn_red(gr0, 3, "s")
-        gj1 = group_tile("gj1")
-        for t in range(T):
-            scatter(banks[t], u00, 0, t, 0, QUART)
-            if t == 1:
-                quant_red(gr0, 0, 1)
-        thermal(w00, 0, 0, 0)
-        turn_slot(j_raw, gj1, 1, 0)
-        turn_slot(j_raw, gj1, 1, 1)
-        thermal(w00, 0, 0, 1)
-        for t in range(T):
-            banks[t] = stage1(0, t, QUART, HALF)
-        turn_slot(j_raw, gj1, 1, 2)
-        turn_slot(j_raw, gj1, 1, 3)
-        for t in range(T):
-            scatter(banks[t], u00, 0, t, QUART, HALF)
-        for t in range(2, T):
-            thermal(w00, 0, 0, t)
-        gr1 = group_tile("gr1")
-        u10 = new_u()
-        w10 = new_w()
-        quant_slot(gj1, j_q[1], 0, 2)
-        turn_red(gr1, 4)
-        turn_red(gr1, 5)
-        turn_red(gr1, 6)
-        turn_red(gr1, 7)
-        quant_slot(gj1, j_q[1], 2, 4)
-        for t in range(T):
-            banks[t] = stage1(1, t, 0, HALF)
-        eta00 = add_eta(u00, w00, 0, HALF)
-        for t in range(T):
-            thermal(w10, 1, 0, t)
-        for t in range(T):
-            scatter(banks[t], u10, 1, t, 0, HALF)
-            if t == 1:
-                quant_eta(eta00, 0, 0, HALF)
-        quant_red(gr1, 1, 0)
-        quant_red(gr1, 1, 1)
-        gl0 = group_tile("gl0")
-        for t in range(T):
-            turn_slot(lam_raw, gl0, 0, t)
-        u01 = new_u()
-        w01 = new_w()
-        gl1 = group_tile("gl1")
-        for t in range(T):
-            banks[t] = stage1(0, t, HALF, D)
-        eta10 = add_eta(u10, w10, 0, HALF)
-        quant_slot(gl0, lam_q[0], 0, 2)
-        quant_slot(gl0, lam_q[0], 2, 4)
-        for t in range(T):
-            thermal(w01, 0, 1, t)
-        for t in range(T):
-            turn_slot(lam_raw, gl1, 1, t)
-        for t in range(T):
-            scatter(banks[t], u01, 0, t, HALF, D)
-            if t == 1:
-                quant_eta(eta10, 1, 0, HALF)
-        u11 = new_u()
-        w11 = new_w()
-        for t in range(T):
-            banks[t] = stage1(1, t, HALF, C2)
-        for t in range(T):
-            thermal(w11, 1, 1, t)
-        quant_slot(gl1, lam_q[1], 0, 2)
-        quant_slot(gl1, lam_q[1], 2, 4)
-        eta01 = add_eta(u01, w01, HALF, D)
-        o0 = [new_o(), new_o()]
-        for q in range(2):
-            for t in range(T):
-                ps = bank("tp")
-                pass2(ps, q, t, 0, 0, HALF)
-                pass2(ps, q, t, 1, 0, HALF)
-                empty(o0[q], ps, t, 0, HALF)
-            store_out(o0[q], q, 0, T, 0, HALF)
-        oq00 = weave(o0[0], 0, HALF, "s")
-        oq10 = weave(o0[1], 0, HALF, "s")
-        for t in range(T):
-            scatter(banks[t], u11, 1, t, HALF, C2)
-            if t == 1:
-                quant_eta(eta01, 0, HALF, D)
-        for t in range(T):
-            banks[t] = stage1(1, t, C2, D)
-        eta11 = add_eta(u11, w11, HALF, C2)
-        for t in range(T):
-            scatter(banks[t], u11, 1, t, C2, D)
-            if t == 1:
-                quant_eta(eta11, 1, HALF, C2)
-        eta11b = add_eta(u11, w11, C2, D)
-        quant_out(oq00, 0, 0, HALF)
+        phi_rows()
+        turn_row("j", 0, 0)
+        phi_inv()
+        turn_red(0)
+        lay_row("j", 0, 0, "s")
+        turn_row("j", 0, 1)
+        lay_red(0, "v")
+        turn_red(1)
+        lay_row("j", 0, 1, "v")
+        turn_row("j", 0, 2)
+        quant_row("j", 0, 0, 1)
+        lay_red(1, "s")
+        turn_red(2)
+        quant_row("j", 0, 1, 2)
+        lay_row("j", 0, 2, "v")
+        turn_row("j", 1, 0)
+        lay_red(2, "s")
+        quant_red(0)
+        turn_red(3)
+        lay_row("j", 1, 0, "v")
+        turn_row("j", 1, 1)
+        lay_red(3, "s")
+        turn_row("j", 0, 3)
+        lay_row("j", 1, 1, "s")
+        quant_red(1)
+        first(0, 0, 0, 256)
+        lay_row("j", 0, 3, "s")
+        quant_row("j", 1, 0, 2)
+        first(0, 1, 0, 256)
+        thermal(0, 0, 0, "s")
+        quant_row("j", 0, 2, 3)
+        turn_row("j", 1, 2)
+        quant_row("j", 0, 3, 4)
+        scatter(0, 0, 0, 256)
+        turn_row("j", 1, 3)
+        scatter(0, 1, 0, 256)
+        lay_row("j", 1, 2, "s")
+        first(0, 0, 256, 512)
+        thermal(0, 0, 1, "v")
+        lay_row("j", 1, 3, "s")
+        first(0, 1, 256, 512)
+        first(0, 2, 0, 256)
+        scatter(0, 0, 256, 512)
+        thermal(0, 0, 2, "s")
+        first(0, 3, 0, 256)
+        scatter(0, 1, 256, 512)
+        first(1, 0, 0, 512)
+        scatter(0, 2, 0, 256)
+        thermal(0, 0, 3, "s")
+        quant_row("j", 1, 2, 4)
+        first(0, 2, 256, 512)
+        first(0, 3, 256, 512)
+        thermal(0, 1, 0, "s")
+        scatter(0, 3, 0, 256)
+        turn_red(4)
+        scatter(0, 2, 256, 512)
+        thermal(0, 1, 1, "s")
+        scatter(0, 3, 256, 512)
+        thermal(1, 0, 0, "s")
+        scatter(1, 0, 0, 512)
+        turn_red(5)
+        thermal(1, 0, 1, "s")
+        add_eta(0, 0, 512)
+        first(1, 1, 0, 512)
+        thermal(1, 0, 2, "s")
+        turn_row("l", 1, 0)
+        lay_red(4, "s")
+        first(1, 2, 0, 512)
+        lay_red(5, "s")
+        turn_row("l", 1, 1)
+        scatter(1, 1, 0, 512)
+        thermal(1, 0, 3, "s")
+        turn_red(6)
+        lay_row("l", 1, 0, "s")
+        scatter(1, 2, 0, 512)
+        turn_row("l", 0, 0)
+        lay_row("l", 1, 1, "s")
+        quant_eta(0, 0, 512)
+        turn_red(7)
+        lay_red(6, "s")
+        quant_red(2)
+        first(1, 3, 0, 512)
+        thermal(0, 1, 2, "s")
+        quant_row("l", 1, 0, 2)
+        first(1, 0, 512, 768)
+        lay_red(7, "s")
+        turn_row("l", 0, 1)
+        scatter(1, 3, 0, 512)
+        lay_row("l", 0, 0, "s")
+        turn_row("l", 1, 2)
+        scatter(1, 0, 512, 768)
+        quant_red(3)
+        thermal(1, 1, 0, "s")
+        turn_row("l", 0, 2)
+        thermal(1, 1, 1, "s")
+        add_eta(1, 0, 512)
+        first(0, 0, 512, 1024)
+        thermal(1, 1, 2, "s")
+        turn_row("l", 1, 3)
+        lay_row("l", 0, 1, "s")
+        lay_row("l", 1, 2, "s")
+        turn_row("l", 0, 3)
+        lay_row("l", 0, 2, "s")
+        scatter(0, 0, 512, 1024)
+        first(0, 1, 512, 1024)
+        lay_row("l", 0, 3, "s")
+        quant_eta(1, 0, 512)
+        first(0, 2, 512, 1024)
+        lay_row("l", 1, 3, "s")
+        quant_row("l", 0, 0, 2)
+        second(1, 0, 0, 512, "tp")
+        thermal(1, 1, 3, "s")
+        scatter(0, 1, 512, 1024)
+        first(0, 3, 512, 1024)
+        thermal(0, 1, 3, "s")
+        scatter(0, 2, 512, 1024)
+        second(0, 0, 0, 512, "tp")
+        empty(1, 0, 0, 512, "s")
+        first(1, 1, 512, 768)
+        scatter(0, 3, 512, 1024)
+        second(1, 1, 0, 512, "tp")
+        empty(0, 0, 0, 512, "s")
+        quant_row("l", 0, 2, 4)
+        second(0, 1, 0, 512, "tp")
+        empty(1, 1, 0, 512, "s")
+        store_out(1, 0, 2, 0, 512)
+        quant_row("l", 1, 2, 4)
+        second(0, 2, 0, 512, "tp")
+        empty(0, 1, 0, 512, "s")
+        store_out(0, 0, 2, 0, 512)
+        scatter(1, 1, 512, 768)
+        second(0, 3, 0, 512, "tp")
+        add_eta(0, 512, 1024)
+        empty(0, 2, 0, 512, "s")
+        first(1, 2, 512, 768)
+        first(1, 0, 768, 1024)
+        empty(0, 3, 0, 512, "s")
+        store_out(0, 2, 4, 0, 512)
+        first(1, 3, 512, 768)
+        second(1, 2, 0, 512, "tp")
+        weave(0, 0, 512, "s")
+        first(1, 1, 768, 1024)
+        second(1, 3, 0, 512, "tp")
+        scatter(1, 2, 512, 768)
+        scatter(1, 3, 512, 768)
+        first(1, 2, 768, 1024)
+        scatter(1, 0, 768, 1024)
+        add_eta(1, 512, 768)
+        first(1, 3, 768, 1024)
+        empty(1, 2, 0, 512, "s")
+        empty(1, 3, 0, 512, "s")
+        store_out(1, 2, 4, 0, 512)
+        quant_eta(0, 512, 1024)
+        weave(1, 0, 512, "s")
+        quant_eta(1, 512, 768)
+        scatter(1, 1, 768, 1024)
+        second(0, 0, 512, 768, "mm")
+        scatter(1, 2, 768, 1024)
+        second(0, 1, 512, 768, "mm")
+        scatter(1, 3, 768, 1024)
+        second(1, 0, 512, 768, "tp")
+        quant_out(0, 0, 512)
         store_codes(0, 0, HALF)
-        quant_eta(eta11b, 1, C2, D)
-        o1 = [new_o(), new_o()]
-        oq1 = {}
-        for q in range(2):
-            for t in range(T):
-                ps = bank("mm" if q == 0 else "tp")
-                pass2(ps, q, t, 0, HALF, C2)
-                pass2(ps, q, t, 1, HALF, C2)
-                empty(o1[q], ps, t, HALF, C2, "s")
-            store_out(o1[q], q, 0, T, HALF, C2)
-        oq1[0, 0] = weave(o1[0], HALF, C2, "v")
-        quant_out(oq10, 1, 0, HALF)
+        second(1, 1, 512, 768, "tp")
+        second(1, 2, 512, 768, "tp")
+        empty(0, 0, 512, 768, "s")
+        second(0, 2, 512, 768, "mm")
+        add_eta(1, 768, 1024)
+        empty(0, 1, 512, 768, "s")
+        store_out(0, 0, 2, 512, 768)
+        second(1, 3, 512, 768, "tp")
+        empty(1, 0, 512, 768, "s")
+        second(0, 3, 512, 768, "mm")
+        empty(1, 1, 512, 768, "s")
+        store_out(1, 0, 2, 512, 768)
+        empty(1, 2, 512, 768, "s")
+        empty(1, 3, 512, 768, "s")
+        store_out(1, 2, 4, 512, 768)
+        quant_eta(1, 768, 1024)
+        empty(0, 3, 512, 768, "s")
+        empty(0, 2, 512, 768, "v")
+        store_out(0, 2, 4, 512, 768)
+        second(0, 0, 768, 1024, "mm")
+        quant_out(1, 0, 512)
         store_codes(1, 0, HALF)
-        store_scales(0, HALF)
-        oq1[1, 0] = weave(o1[1], HALF, C2, "s")
-        quant_out(oq1[0, 0], 0, HALF, C2)
-        for q in range(2):
-            for t in range(T):
-                ps = bank("mm" if q == 0 else "tp")
-                pass2(ps, q, t, 0, C2, D)
-                pass2(ps, q, t, 1, C2, D)
-                empty(o1[q], ps, t, C2, D, "s" if q == 0 else "v")
-            store_out(o1[q], q, 0, T, C2, D)
-        quant_out(oq1[1, 0], 1, HALF, C2)
-        oq1[0, 1] = weave(o1[0], C2, D, "s")
-        oq1[1, 1] = weave(o1[1], C2, D, "v")
-        quant_out(oq1[1, 1], 1, C2, D)
-        store_codes(1, HALF, D)
-        quant_out(oq1[0, 1], 0, C2, D)
+        second(0, 1, 768, 1024, "mm")
+        second(1, 0, 768, 1024, "tp")
+        empty(0, 0, 768, 1024, "s")
+        weave(1, 512, 768, "v")
+        second(0, 2, 768, 1024, "mm")
+        empty(0, 1, 768, 1024, "s")
+        store_out(0, 0, 2, 768, 1024)
+        second(0, 3, 768, 1024, "mm")
+        second(1, 1, 768, 1024, "tp")
+        empty(0, 2, 768, 1024, "s")
+        weave(0, 512, 768, "v")
+        second(1, 2, 768, 1024, "tp")
+        empty(0, 3, 768, 1024, "s")
+        store_out(0, 2, 4, 768, 1024)
+        second(1, 3, 768, 1024, "tp")
+        empty(1, 1, 768, 1024, "s")
+        empty(1, 0, 768, 1024, "v")
+        store_out(1, 0, 2, 768, 1024)
+        empty(1, 2, 768, 1024, "s")
+        weave(0, 768, 1024, "v")
+        empty(1, 3, 768, 1024, "s")
+        store_out(1, 2, 4, 768, 1024)
+        weave(1, 768, 1024, "s")
+        quant_out(0, 512, 768)
+        quant_out(0, 768, 1024)
         store_codes(0, HALF, D)
-        store_scales(HALF, D)
+        quant_out(1, 512, 768)
+        quant_out(1, 768, 1024)
+        store_codes(1, HALF, D)
+        store_scales(0, D)

@@ -18,6 +18,7 @@ T = 4
 G = 2
 HALF = 512
 QUART = 256
+THREE = HALF + QUART
 FLOPS = 2 * 2 * D * D * D
 
 
@@ -53,33 +54,31 @@ def tile_redistributedsourcesharedoperatorstep_kernel(
             rows = src[HALF * g : HALF * (g + 1), :].rearrange("(p t) k -> p t k", t=T)
             nc.sync.dma_start(out=dst[g][:, t0:t1, c0:c1], in_=rows[:, t0:t1, c0:c1])
 
+        for i in range(2):
+            load_red(i)
         load_rows(j_raw, j, 0, 0, 1)
-        load_red(0)
-        load_rows(j_raw, j, 0, 1, 2)
-        load_red(1)
-        load_rows(j_raw, j, 0, 2, 3)
-        load_red(2)
-        load_rows(j_raw, j, 1, 0, 2)
-        load_red(3)
-        load_rows(j_raw, j, 0, 3, 4)
+        for i in range(2, 4):
+            load_red(i)
+        for t in range(1, T):
+            load_rows(j_raw, j, 0, t, t + 1)
         load_rows(b_raw, b, 0, 0, T, 0, HALF)
+        load_rows(j_raw, j, 1, 0, 2)
         load_rows(j_raw, j, 1, 2, 4)
+        for i in range(4, 6):
+            load_red(i)
         load_rows(b_raw, b, 1, 0, T, 0, HALF)
-        load_rows(b_raw, b, 0, 0, T, HALF, D)
-        load_red(4)
-        load_rows(lam_raw, lam, 1, 0, 2)
-        load_red(5)
-        load_rows(lam_raw, lam, 1, 2, 4)
-        load_rows(lam_raw, lam, 0, 0, 2)
-        load_red(6)
-        load_red(7)
-        load_rows(b_raw, b, 1, 0, T, HALF, D)
-        load_rows(lam_raw, lam, 0, 2, 4)
+        for i in range(6, 8):
+            load_red(i)
+        for g in range(G):
+            load_rows(b_raw, b, g, 0, T, HALF, D)
+        for g in (1, 0):
+            load_rows(lam_raw, lam, g, 0, 2)
+            load_rows(lam_raw, lam, g, 2, 4)
 
         ident = keep.tile([P, P], F32, name="ident")
         make_identity(nc, ident[:])
-        ident_bf = keep.tile([P, P], BF16, name="ident_bf")
-        nc.vector.tensor_copy(out=ident_bf[:], in_=ident[:])
+        inv_col = keep.tile([P, 8], F32, name="inv_col")
+        nc.vector.reciprocal(out=inv_col[:], in_=phi_sb[:])
 
         fac_a = keep.tile([P, G * T], F32, name="fac_a")
         fac_b = keep.tile([P, G * T], F32, name="fac_b")
@@ -125,16 +124,15 @@ def tile_redistributedsourcesharedoperatorstep_kernel(
             return tile_of("grp", key, [T * D], BF16, 4, 64)
 
         def phi_rows():
-            ps = psum.tile([P, D], BF16, name="phi_ps", tag="mm")
-            for i in range(8):
-                nc.tensor.transpose(ps[:, P * i : P * (i + 1)], phi_sb[:, i : i + 1].to_broadcast([P, P]), ident_bf[:])
-            banks["phi"] = ps
+            for half in range(2):
+                ps = bank(("phi", half), "mm")
+                for i in range(4):
+                    col = inv_col[:, 4 * half + i : 4 * half + i + 1]
+                    nc.tensor.transpose(ps[:, P * i : P * (i + 1)], col.to_broadcast([P, P]), ident[:])
 
-        def phi_inv():
-            nc.vector.reciprocal(
-                out=inv_phi[:].rearrange("p (k i) -> p k i", i=8),
-                in_=banks["phi"][:].rearrange("p (i k) -> p k i", i=8),
-            )
+        def phi_copy(half, eng):
+            dst = inv_phi[:].rearrange("p (k i) -> p k i", i=8)[:, :, 4 * half : 4 * half + 4]
+            copy(eng, dst, banks["phi", half][:].rearrange("p (i k) -> p k i", i=4))
 
         def turn(key, src):
             ps = bank(key, "tp")
@@ -290,217 +288,106 @@ def tile_redistributedsourcesharedoperatorstep_kernel(
                 )
 
         phi_rows()
-        turn_row("j", 0, 0)
-        phi_inv()
-        turn_red(0)
-        lay_row("j", 0, 0, "s")
-        turn_row("j", 0, 1)
-        lay_red(0, "v")
-        turn_red(1)
-        lay_row("j", 0, 1, "v")
-        turn_row("j", 0, 2)
-        quant_row("j", 0, 0, 1)
-        lay_red(1, "s")
-        turn_red(2)
-        quant_row("j", 0, 1, 2)
-        lay_row("j", 0, 2, "v")
-        turn_row("j", 1, 0)
-        lay_red(2, "s")
+        phi_copy(0, "v")
+        phi_copy(1, "v")
+        for i in range(T):
+            turn_red(i)
+            lay_red(i, "s")
         quant_red(0)
-        turn_red(3)
-        lay_row("j", 1, 0, "v")
-        turn_row("j", 1, 1)
-        lay_red(3, "s")
-        turn_row("j", 0, 3)
-        lay_row("j", 1, 1, "s")
         quant_red(1)
-        first(0, 0, 0, 256)
-        lay_row("j", 0, 3, "s")
-        quant_row("j", 1, 0, 2)
-        first(0, 1, 0, 256)
-        thermal(0, 0, 0, "s")
-        quant_row("j", 0, 2, 3)
-        turn_row("j", 1, 2)
-        quant_row("j", 0, 3, 4)
-        scatter(0, 0, 0, 256)
+        for t in range(T):
+            turn_row("j", 0, t)
+            lay_row("j", 0, t, "s")
+            quant_row("j", 0, t, t + 1)
+        for t in range(T):
+            first(0, t, 0, HALF)
+            thermal(0, 0, t, "s")
+            scatter(0, t, 0, HALF)
+        for t in range(3):
+            turn_row("j", 1, t)
+            lay_row("j", 1, t, "v" if t == 1 else "s")
+        for i in range(4, 6):
+            turn_red(i)
+            lay_red(i, "s")
         turn_row("j", 1, 3)
-        scatter(0, 1, 0, 256)
-        lay_row("j", 1, 2, "s")
-        first(0, 0, 256, 512)
-        thermal(0, 0, 1, "v")
         lay_row("j", 1, 3, "s")
-        first(0, 1, 256, 512)
-        first(0, 2, 0, 256)
-        scatter(0, 0, 256, 512)
-        thermal(0, 0, 2, "s")
-        first(0, 3, 0, 256)
-        scatter(0, 1, 256, 512)
-        first(1, 0, 0, 512)
-        scatter(0, 2, 0, 256)
-        thermal(0, 0, 3, "s")
+        quant_row("j", 1, 0, 2)
+        add_eta(0, 0, HALF)
         quant_row("j", 1, 2, 4)
-        first(0, 2, 256, 512)
-        first(0, 3, 256, 512)
-        thermal(0, 1, 0, "s")
-        scatter(0, 3, 0, 256)
-        turn_red(4)
-        scatter(0, 2, 256, 512)
-        thermal(0, 1, 1, "s")
-        scatter(0, 3, 256, 512)
-        thermal(1, 0, 0, "s")
-        scatter(1, 0, 0, 512)
-        turn_red(5)
-        thermal(1, 0, 1, "s")
-        add_eta(0, 0, 512)
-        first(1, 1, 0, 512)
-        thermal(1, 0, 2, "s")
-        turn_row("l", 1, 0)
-        lay_red(4, "s")
-        first(1, 2, 0, 512)
-        lay_red(5, "s")
-        turn_row("l", 1, 1)
-        scatter(1, 1, 0, 512)
-        thermal(1, 0, 3, "s")
-        turn_red(6)
-        lay_row("l", 1, 0, "s")
-        scatter(1, 2, 0, 512)
-        turn_row("l", 0, 0)
-        lay_row("l", 1, 1, "s")
-        quant_eta(0, 0, 512)
-        turn_red(7)
-        lay_red(6, "s")
         quant_red(2)
-        first(1, 3, 0, 512)
-        thermal(0, 1, 2, "s")
-        quant_row("l", 1, 0, 2)
-        first(1, 0, 512, 768)
-        lay_red(7, "s")
-        turn_row("l", 0, 1)
-        scatter(1, 3, 0, 512)
-        lay_row("l", 0, 0, "s")
-        turn_row("l", 1, 2)
-        scatter(1, 0, 512, 768)
+        for t in range(T):
+            first(1, t, 0, HALF)
+            thermal(1, 0, t, "s")
+            scatter(1, t, 0, HALF)
+        quant_eta(0, 0, HALF)
+        for i in range(6, 8):
+            turn_red(i)
+        for t in range(T):
+            first(1, t, HALF, THREE)
+            thermal(0, 1, t, "s")
+            scatter(1, t, HALF, THREE)
+        for i in range(6, 8):
+            lay_red(i, "s")
         quant_red(3)
-        thermal(1, 1, 0, "s")
-        turn_row("l", 0, 2)
-        thermal(1, 1, 1, "s")
-        add_eta(1, 0, 512)
-        first(0, 0, 512, 1024)
-        thermal(1, 1, 2, "s")
-        turn_row("l", 1, 3)
-        lay_row("l", 0, 1, "s")
-        lay_row("l", 1, 2, "s")
-        turn_row("l", 0, 3)
-        lay_row("l", 0, 2, "s")
-        scatter(0, 0, 512, 1024)
-        first(0, 1, 512, 1024)
-        lay_row("l", 0, 3, "s")
-        quant_eta(1, 0, 512)
-        first(0, 2, 512, 1024)
-        lay_row("l", 1, 3, "s")
-        quant_row("l", 0, 0, 2)
-        second(1, 0, 0, 512, "tp")
-        thermal(1, 1, 3, "s")
-        scatter(0, 1, 512, 1024)
-        first(0, 3, 512, 1024)
-        thermal(0, 1, 3, "s")
-        scatter(0, 2, 512, 1024)
-        second(0, 0, 0, 512, "tp")
-        empty(1, 0, 0, 512, "s")
-        first(1, 1, 512, 768)
-        scatter(0, 3, 512, 1024)
-        second(1, 1, 0, 512, "tp")
-        empty(0, 0, 0, 512, "s")
-        quant_row("l", 0, 2, 4)
-        second(0, 1, 0, 512, "tp")
-        empty(1, 1, 0, 512, "s")
-        store_out(1, 0, 2, 0, 512)
-        quant_row("l", 1, 2, 4)
-        second(0, 2, 0, 512, "tp")
-        empty(0, 1, 0, 512, "s")
-        store_out(0, 0, 2, 0, 512)
-        scatter(1, 1, 512, 768)
-        second(0, 3, 0, 512, "tp")
-        add_eta(0, 512, 1024)
-        empty(0, 2, 0, 512, "s")
-        first(1, 2, 512, 768)
-        first(1, 0, 768, 1024)
-        empty(0, 3, 0, 512, "s")
-        store_out(0, 2, 4, 0, 512)
-        first(1, 3, 512, 768)
-        second(1, 2, 0, 512, "tp")
-        weave(0, 0, 512, "s")
-        first(1, 1, 768, 1024)
-        second(1, 3, 0, 512, "tp")
-        scatter(1, 2, 512, 768)
-        scatter(1, 3, 512, 768)
-        first(1, 2, 768, 1024)
-        scatter(1, 0, 768, 1024)
-        add_eta(1, 512, 768)
-        first(1, 3, 768, 1024)
-        empty(1, 2, 0, 512, "s")
-        empty(1, 3, 0, 512, "s")
-        store_out(1, 2, 4, 0, 512)
-        quant_eta(0, 512, 1024)
-        weave(1, 0, 512, "s")
-        quant_eta(1, 512, 768)
-        scatter(1, 1, 768, 1024)
-        second(0, 0, 512, 768, "mm")
-        scatter(1, 2, 768, 1024)
-        second(0, 1, 512, 768, "mm")
-        scatter(1, 3, 768, 1024)
-        second(1, 0, 512, 768, "tp")
-        quant_out(0, 0, 512)
-        store_codes(0, 0, HALF)
-        second(1, 1, 512, 768, "tp")
-        second(1, 2, 512, 768, "tp")
-        empty(0, 0, 512, 768, "s")
-        second(0, 2, 512, 768, "mm")
-        add_eta(1, 768, 1024)
-        empty(0, 1, 512, 768, "s")
-        store_out(0, 0, 2, 512, 768)
-        second(1, 3, 512, 768, "tp")
-        empty(1, 0, 512, 768, "s")
-        second(0, 3, 512, 768, "mm")
-        empty(1, 1, 512, 768, "s")
-        store_out(1, 0, 2, 512, 768)
-        empty(1, 2, 512, 768, "s")
-        empty(1, 3, 512, 768, "s")
-        store_out(1, 2, 4, 512, 768)
-        quant_eta(1, 768, 1024)
-        empty(0, 3, 512, 768, "s")
-        empty(0, 2, 512, 768, "v")
-        store_out(0, 2, 4, 512, 768)
-        second(0, 0, 768, 1024, "mm")
-        quant_out(1, 0, 512)
+        add_eta(1, 0, HALF)
+        for t in range(T):
+            thermal(1, 1, t, "s")
+        for t in range(T):
+            turn_row("l", 1, t)
+            lay_row("l", 1, t, "s")
+        for t in range(T):
+            first(0, t, HALF, D)
+        for t in range(2):
+            scatter(0, t, HALF, D)
+        quant_eta(1, 0, HALF)
+        for t in (0, 2):
+            quant_row("l", 1, t, t + 2)
+        for t in range(2, T):
+            scatter(0, t, HALF, D)
+        for t in range(T):
+            turn_row("l", 0, t)
+            lay_row("l", 0, t, "s")
+        for t in (0, 2):
+            quant_row("l", 0, t, t + 2)
+        add_eta(1, HALF, THREE)
+        add_eta(0, HALF, D)
+        quant_eta(1, HALF, THREE)
+        quant_eta(0, HALF, D)
+        for q in (1, 0):
+            for t in range(T):
+                second(q, t, 0, HALF, "tp")
+                empty(q, t, 0, HALF, "s")
+                if t % 2:
+                    store_out(q, t - 1, t + 1, 0, HALF)
+        weave(1, 0, HALF, "s")
+        for t in range(T):
+            first(1, t, THREE, D)
+            scatter(1, t, THREE, D)
+        add_eta(1, THREE, D)
+        quant_eta(1, THREE, D)
+        quant_out(1, 0, HALF)
+        weave(0, 0, HALF, "v")
+        for q in range(G):
+            for t in range(T):
+                second(q, t, HALF, THREE, "tp" if q else "mm")
+                empty(q, t, HALF, THREE, "s")
+                if t % 2:
+                    store_out(q, t - 1, t + 1, HALF, THREE)
         store_codes(1, 0, HALF)
-        second(0, 1, 768, 1024, "mm")
-        second(1, 0, 768, 1024, "tp")
-        empty(0, 0, 768, 1024, "s")
-        weave(1, 512, 768, "v")
-        second(0, 2, 768, 1024, "mm")
-        empty(0, 1, 768, 1024, "s")
-        store_out(0, 0, 2, 768, 1024)
-        second(0, 3, 768, 1024, "mm")
-        second(1, 1, 768, 1024, "tp")
-        empty(0, 2, 768, 1024, "s")
-        weave(0, 512, 768, "v")
-        second(1, 2, 768, 1024, "tp")
-        empty(0, 3, 768, 1024, "s")
-        store_out(0, 2, 4, 768, 1024)
-        second(1, 3, 768, 1024, "tp")
-        empty(1, 1, 768, 1024, "s")
-        empty(1, 0, 768, 1024, "v")
-        store_out(1, 0, 2, 768, 1024)
-        empty(1, 2, 768, 1024, "s")
-        weave(0, 768, 1024, "v")
-        empty(1, 3, 768, 1024, "s")
-        store_out(1, 2, 4, 768, 1024)
-        weave(1, 768, 1024, "s")
-        quant_out(0, 512, 768)
-        quant_out(0, 768, 1024)
-        store_codes(0, HALF, D)
-        quant_out(1, 512, 768)
-        quant_out(1, 768, 1024)
+        weave(0, HALF, THREE, "v")
+        quant_out(0, 0, HALF)
+        for q in (1, 0):
+            for t in range(T):
+                second(q, t, THREE, D, "tp" if q else "mm")
+                empty(q, t, THREE, D, "v" if (q, t) == (0, 3) else "s")
+                if t % 2:
+                    store_out(q, t - 1, t + 1, THREE, D)
+        store_codes(0, 0, HALF)
+        weave(1, HALF, THREE, "v")
+        weave(1, THREE, D, "s")
+        weave(0, THREE, D, "s")
+        for c0, c1, q in ((THREE, D, 1), (HALF, THREE, 1), (HALF, THREE, 0), (THREE, D, 0)):
+            quant_out(q, c0, c1)
         store_codes(1, HALF, D)
+        store_codes(0, HALF, D)
         store_scales(0, D)

from contextlib import ExitStack

import concourse.mybir as mybir
from concourse.masks import make_identity

F32 = mybir.dt.float32
BF16 = mybir.dt.bfloat16
U32 = mybir.dt.uint32
I32 = mybir.dt.int32
U8 = mybir.dt.uint8
FP8X4 = mybir.dt.float8_e4m3fn_x4
ALU = mybir.AluOpType
ACT = mybir.ActivationFunctionType

P = 128
D = 1024
T = 4
G = 2
HALF = 512
QUART = 256
THREE = HALF + QUART
FLOPS = 2 * 2 * D * D * D


def tile_redistributedsourcesharedoperatorstep_kernel(
    tc, j, red, phi, eps, b, kappa, lam, out_0, out_1, out_2
):
    nc = tc.nc
    with ExitStack() as ctx:
        keep = ctx.enter_context(tc.tile_pool(name="keep", bufs=1))
        stage = ctx.enter_context(tc.tile_pool(name="stage", bufs=2))
        psum = ctx.enter_context(tc.psum_pool(name="psum", bufs=4))
        ctx.enter_context(tc.manual_schedule())

        phi_sb = keep.tile([P, 8], BF16, name="phi_sb")
        eps_sb = keep.tile([P, G * T], BF16, name="eps_sb")
        kap_sb = keep.tile([P, G * T], BF16, name="kap_sb")
        nc.scalar.dma_start(out=phi_sb[:], in_=phi.rearrange("(k i) -> k i", i=8))
        for dst, src in ((eps_sb, eps), (kap_sb, kappa)):
            nc.scalar.dma_start(
                out=dst[:].rearrange("p (g t) -> p g t", g=G),
                in_=src.rearrange("(g p t) -> p g t", g=G, t=T),
            )

        red_raw = [stage.tile([P, T, D], BF16, name=f"red_raw{h}", tag="rows", bufs=8) for h in range(2)]
        j_raw = [stage.tile([P, T, D], BF16, name=f"j_raw{g}", tag="rows", bufs=8) for g in range(G)]
        lam_raw = [stage.tile([P, T, D], BF16, name=f"lam_raw{g}", tag="rows", bufs=8) for g in range(G)]
        b_raw = [stage.tile([P, T, D], BF16, name=f"b_raw{g}", tag="rows", bufs=8) for g in range(G)]

        def load_red(i):
            nc.sync.dma_start(out=red_raw[i // T][:, i % T, :], in_=red[P * i : P * (i + 1), :])

        def load_rows(dst, src, g, t0, t1, c0=0, c1=D):
            rows = src[HALF * g : HALF * (g + 1), :].rearrange("(p t) k -> p t k", t=T)
            nc.sync.dma_start(out=dst[g][:, t0:t1, c0:c1], in_=rows[:, t0:t1, c0:c1])

        for i in range(2):
            load_red(i)
        load_rows(j_raw, j, 0, 0, 1)
        for i in range(2, 4):
            load_red(i)
        for t in range(1, T):
            load_rows(j_raw, j, 0, t, t + 1)
        load_rows(b_raw, b, 0, 0, T, 0, HALF)
        load_rows(j_raw, j, 1, 0, 2)
        load_rows(j_raw, j, 1, 2, 4)
        for i in range(4, 6):
            load_red(i)
        load_rows(b_raw, b, 1, 0, T, 0, HALF)
        for i in range(6, 8):
            load_red(i)
        for g in range(G):
            load_rows(b_raw, b, g, 0, T, HALF, D)
        for g in (1, 0):
            load_rows(lam_raw, lam, g, 0, 2)
            load_rows(lam_raw, lam, g, 2, 4)

        ident = keep.tile([P, P], F32, name="ident")
        make_identity(nc, ident[:])
        inv_col = keep.tile([P, 8], F32, name="inv_col")
        nc.vector.reciprocal(out=inv_col[:], in_=phi_sb[:])

        fac_a = keep.tile([P, G * T], F32, name="fac_a")
        fac_b = keep.tile([P, G * T], F32, name="fac_b")
        one_m = keep.tile([P, G * T], F32, name="one_m")
        nc.gpsimd.tensor_scalar(out=one_m[:], in0=eps_sb[:], scalar1=-1.0, scalar2=1.0, op0=ALU.mult, op1=ALU.add)
        nc.gpsimd.tensor_tensor(out=fac_a[:], in0=kap_sb[:], in1=one_m[:], op=ALU.mult)
        nc.gpsimd.tensor_tensor(out=fac_b[:], in0=kap_sb[:], in1=eps_sb[:], op=ALU.mult)
        inv_phi = keep.tile([P, D], F32, name="inv_phi")

        def codes(name, shape):
            c = keep.tile([P] + shape, U32, name=name + "_c", align_bytes=64)
            s = keep.tile([P] + shape, U8, name=name + "_s", align_bytes=64)
            return c, s

        red_q = [codes(f"red{h}", [G, HALF]) for h in range(2)]
        row_q = {}
        for m in "jl":
            for g in range(G):
                row_q[m, g] = codes(f"{m}{g}", [T, G, P])
        eta_q = [codes(f"eta{g}", [D]) for g in range(G)]
        out_c = [keep.tile([P, D], U32, name=f"out_c{g}", align_bytes=64) for g in range(G)]
        out_s = keep.tile([P, G, D], U8, name="out_s", align_bytes=64)

        def copy(eng, out, in_):
            if eng == "s":
                nc.scalar.copy(out=out, in_=in_)
            else:
                nc.vector.tensor_copy(out=out, in_=in_)

        banks = {}
        tiles = {}

        def bank(key, tag):
            banks[key] = psum.tile([P, HALF], F32, name="bank", tag=tag)
            return banks[key]

        def tile_of(kind, key, shape, dtype, bufs, align=None):
            if (kind, key) not in tiles:
                tiles[kind, key] = stage.tile([P] + shape, dtype, name=kind, tag=kind, bufs=bufs, align_bytes=align)
            return tiles[kind, key]

        def grouped(key):
            return tile_of("grp", key, [T * D], BF16, 4, 64)

        def phi_rows():
            for half in range(2):
                ps = bank(("phi", half), "mm")
                for i in range(4):
                    col = inv_col[:, 4 * half + i : 4 * half + i + 1]
                    nc.tensor.transpose(ps[:, P * i : P * (i + 1)], col.to_broadcast([P, P]), ident[:])

        def phi_copy(half, eng):
            dst = inv_phi[:].rearrange("p (k i) -> p k i", i=8)[:, :, 4 * half : 4 * half + 4]
            copy(eng, dst, banks["phi", half][:].rearrange("p (i k) -> p k i", i=4))

        def turn(key, src):
            ps = bank(key, "tp")
            words = src.bitcast(F32)
            for g in range(G):
                for u in range(2):
                    o = P * (2 * g + u)
                    nc.tensor.transpose(ps[:, o : o + P], words[:, 256 * g + u : 256 * (g + 1) : 2], ident[:])

        def lay(key, dst, eng):
            copy(eng, dst, banks[key][:].rearrange("p (g u r) -> p g r u", g=G, u=2))

        def turn_red(i):
            turn(("r", i), red_raw[i // T][:, i % T, :])

        def lay_red(i, eng):
            dst = grouped(("r", i // T))[:].bitcast(F32).rearrange("p (g n u) -> p g n u", g=G, u=2)
            lay(("r", i), dst[:, :, P * (i % T) : P * (i % T + 1), :], eng)

        def quant_red(pair):
            h = pair // 2
            src = grouped(("r", h))[:].rearrange("p (g w) -> p g w", g=G)
            c0 = QUART * (pair % 2)
            for g in range(G):
                nc.vector.quantize_mx(
                    out=red_q[h][0][:, g, c0 : c0 + QUART].bitcast(FP8X4),
                    scales=red_q[h][1][:, g, c0 : c0 + QUART],
                    in_=src[:, g, T * c0 : T * (c0 + QUART)],
                )

        def turn_row(m, g, t):
            turn((m, g, t), (j_raw if m == "j" else lam_raw)[g][:, t, :])

        def lay_row(m, g, t, eng):
            dst = grouped((m, g))[:].bitcast(F32).rearrange("p (t g n u) -> p t g n u", t=T, g=G, u=2)
            lay((m, g, t), dst[:, t, :, :, :], eng)

        def quant_row(m, g, t0, t1):
            q = row_q[m, g]
            nc.vector.quantize_mx(
                out=q[0][:, t0:t1].rearrange("p t g m -> p (t g m)").bitcast(FP8X4),
                scales=q[1][:, t0:t1].rearrange("p t g m -> p (t g m)"),
                in_=grouped((m, g))[:, D * t0 : D * t1],
            )

        def first(r, t, c0, c1):
            ps = bank(("m", r, t, c0), "mm")
            h = c0 // HALF
            cols = slice(c0 - HALF * h, c1 - HALF * h)
            q = row_q["j", r]
            for g in range(G):
                nc.tensor.matmul_mx(
                    out=ps[:, : c1 - c0],
                    lhsT=q[0][:, t, g, :].bitcast(FP8X4),
                    lhsT_scale=q[1][:, t, g, :],
                    rhs=red_q[h][0][:, g, cols].bitcast(FP8X4),
                    rhs_scale=red_q[h][1][:, g, cols],
                    start=(g == 0),
                    stop=(g == G - 1),
                )

        def scatter(r, t, c0, c1):
            h = c0 // HALF
            u = tile_of("u", (r, h), [T, HALF], F32, 3)
            nc.vector.scalar_tensor_tensor(
                out=u[:, t, c0 - HALF * h : c1 - HALF * h],
                in0=banks["m", r, t, c0][:, : c1 - c0],
                scalar=fac_a[:, T * r + t : T * r + t + 1],
                in1=inv_phi[:, c0:c1],
                op0=ALU.mult,
                op1=ALU.mult,
            )

        def thermal(r, h, t, eng):
            w = tile_of("w", (r, h), [T, HALF], F32, 3)
            factor = fac_b[:, T * r + t : T * r + t + 1]
            src = b_raw[r][:, t, HALF * h : HALF * (h + 1)]
            if eng == "s":
                nc.scalar.activation(out=w[:, t, :], in_=src, func=ACT.Copy, scale=factor)
            else:
                nc.vector.tensor_scalar(out=w[:, t, :], in0=src, scalar1=factor, scalar2=None, op0=ALU.mult)

        def add_eta(r, c0, c1):
            h = c0 // HALF
            cols = slice(c0 - HALF * h, c1 - HALF * h)
            eta = tile_of("eta", (r, c0), [HALF * T], BF16, 2, 64)
            nc.vector.tensor_tensor(
                out=eta[:, : T * (c1 - c0)].rearrange("p (c i t) -> p c t i", i=4, t=T),
                in0=tiles["u", (r, h)][:, :, cols].rearrange("p t (c i) -> p c t i", i=4),
                in1=tiles["w", (r, h)][:, :, cols].rearrange("p t (c i) -> p c t i", i=4),
                op=ALU.add,
            )

        def quant_eta(r, c0, c1):
            nc.vector.quantize_mx(
                out=eta_q[r][0][:, c0:c1].bitcast(FP8X4),
                scales=eta_q[r][1][:, c0:c1],
                in_=tiles["eta", (r, c0)][:, : T * (c1 - c0)],
            )

        def second(q, t, c0, c1, tag):
            ps = bank(("p", q, t, c0), tag)
            lam8 = row_q["l", q]
            for r in range(G):
                nc.tensor.matmul_mx(
                    out=ps[:, : c1 - c0],
                    lhsT=lam8[0][:, t, r, :].bitcast(FP8X4),
                    lhsT_scale=lam8[1][:, t, r, :],
                    rhs=eta_q[r][0][:, c0:c1].bitcast(FP8X4),
                    rhs_scale=eta_q[r][1][:, c0:c1],
                    start=(r == 0),
                    stop=(r == G - 1),
                )

        def result(q, c0):
            return tile_of("rows", (q, c0 // HALF), [T, HALF], F32, 8)

        def empty(q, t, c0, c1, eng):
            o = result(q, c0)
            copy(eng, o[:, t, c0 % HALF : c0 % HALF + c1 - c0], banks["p", q, t, c0][:, : c1 - c0])

        def store_out(q, t0, t1, c0, c1):
            rows = out_0[HALF * q : HALF * (q + 1), :].rearrange("(p t) n -> p t n", t=T)
            nc.sync.dma_start(out=rows[:, t0:t1, c0:c1], in_=result(q, c0)[:, t0:t1, c0 % HALF : c0 % HALF + c1 - c0])

        def weave(q, c0, c1, eng):
            n = c1 - c0
            oq = tile_of("oq", (q, c0), [HALF * T], BF16, 4, 64)
            copy(
                eng,
                oq[:, : T * n].rearrange("p (c i t) -> p c t i", i=4, t=T),
                result(q, c0)[:, :, c0 % HALF : c0 % HALF + n].rearrange("p t (c i) -> p c t i", i=4),
            )

        def quant_out(q, c0, c1):
            nc.vector.quantize_mx(
                out=out_c[q][:, c0:c1].bitcast(FP8X4),
                scales=out_s[:, q, c0:c1],
                in_=tiles["oq", (q, c0)][:, : T * (c1 - c0)],
            )

        def store_codes(q, c0, c1):
            nc.sync.dma_start(
                out=out_1[q].rearrange("p m t -> p (m t)").bitcast(I32)[:, c0:c1],
                in_=out_c[q][:, c0:c1].bitcast(I32),
            )

        def store_scales(c0, c1):
            for quad in range(4):
                nc.sync.dma_start(
                    out=out_2[:, 4 * quad : 4 * quad + 4, c0:c1].rearrange("g q n -> q g n").bitcast(I32),
                    in_=out_s[32 * quad : 32 * quad + 4, :, c0:c1].bitcast(I32),
                )

        phi_rows()
        phi_copy(0, "v")
        phi_copy(1, "v")
        for i in range(T):
            turn_red(i)
            lay_red(i, "s")
        quant_red(0)
        quant_red(1)
        for t in range(T):
            turn_row("j", 0, t)
            lay_row("j", 0, t, "s")
            quant_row("j", 0, t, t + 1)
        for t in range(T):
            first(0, t, 0, HALF)
            thermal(0, 0, t, "s")
            scatter(0, t, 0, HALF)
        for t in range(3):
            turn_row("j", 1, t)
            lay_row("j", 1, t, "v" if t == 1 else "s")
        for i in range(4, 6):
            turn_red(i)
            lay_red(i, "s")
        turn_row("j", 1, 3)
        lay_row("j", 1, 3, "s")
        quant_row("j", 1, 0, 2)
        add_eta(0, 0, HALF)
        quant_row("j", 1, 2, 4)
        quant_red(2)
        for t in range(T):
            first(1, t, 0, HALF)
            thermal(1, 0, t, "s")
            scatter(1, t, 0, HALF)
        quant_eta(0, 0, HALF)
        for i in range(6, 8):
            turn_red(i)
        for t in range(T):
            first(1, t, HALF, THREE)
            thermal(0, 1, t, "s")
            scatter(1, t, HALF, THREE)
        for i in range(6, 8):
            lay_red(i, "s")
        quant_red(3)
        add_eta(1, 0, HALF)
        for t in range(T):
            thermal(1, 1, t, "s")
        for t in range(T):
            turn_row("l", 1, t)
            lay_row("l", 1, t, "s")
        for t in range(T):
            first(0, t, HALF, D)
        for t in range(2):
            scatter(0, t, HALF, D)
        quant_eta(1, 0, HALF)
        for t in (0, 2):
            quant_row("l", 1, t, t + 2)
        for t in range(2, T):
            scatter(0, t, HALF, D)
        for t in range(T):
            turn_row("l", 0, t)
            lay_row("l", 0, t, "s")
        for t in (0, 2):
            quant_row("l", 0, t, t + 2)
        add_eta(1, HALF, THREE)
        add_eta(0, HALF, D)
        quant_eta(1, HALF, THREE)
        quant_eta(0, HALF, D)
        for q in (1, 0):
            for t in range(T):
                second(q, t, 0, HALF, "tp")
                empty(q, t, 0, HALF, "s")
                if t % 2:
                    store_out(q, t - 1, t + 1, 0, HALF)
        weave(1, 0, HALF, "s")
        for t in range(T):
            first(1, t, THREE, D)
            scatter(1, t, THREE, D)
        add_eta(1, THREE, D)
        quant_eta(1, THREE, D)
        quant_out(1, 0, HALF)
        weave(0, 0, HALF, "v")
        for q in range(G):
            for t in range(T):
                second(q, t, HALF, THREE, "tp" if q else "mm")
                empty(q, t, HALF, THREE, "s")
                if t % 2:
                    store_out(q, t - 1, t + 1, HALF, THREE)
        store_codes(1, 0, HALF)
        weave(0, HALF, THREE, "v")
        quant_out(0, 0, HALF)
        for q in (1, 0):
            for t in range(T):
                second(q, t, THREE, D, "tp" if q else "mm")
                empty(q, t, THREE, D, "v" if (q, t) == (0, 3) else "s")
                if t % 2:
                    store_out(q, t - 1, t + 1, THREE, D)
        store_codes(0, 0, HALF)
        weave(1, HALF, THREE, "v")
        weave(1, THREE, D, "s")
        weave(0, THREE, D, "s")
        for c0, c1, q in ((THREE, D, 1), (HALF, THREE, 1), (HALF, THREE, 0), (THREE, D, 0)):
            quant_out(q, c0, c1)
        store_codes(1, HALF, D)
        store_codes(0, HALF, D)
        store_scales(0, D)
